import numpy as np
import ml_dtypes


def mxq(x, axis, fmt="e4m3"):
    dtype, down = {"e4m3": (ml_dtypes.float8_e4m3fn, 7), "e5m2": (ml_dtypes.float8_e5m2, 14)}[fmt]
    v = np.moveaxis(np.asarray(x, np.float32).astype(ml_dtypes.bfloat16).astype(np.float64), axis, -1)
    blocks = v.reshape(v.shape[:-1] + (-1, 32))
    amax = np.abs(blocks).max(-1, keepdims=True)
    byte = np.maximum(np.where(amax > 0, np.frexp(amax)[1] - 1 + 127, 0) - down, 1)
    scale = np.exp2(byte - 127.0)
    codes = (blocks / scale).astype(np.float32).astype(dtype).astype(np.float64)
    return np.moveaxis((codes * scale).reshape(v.shape), -1, axis)


WIDE = False


def mx_kscale(k):
    if not WIDE:
        return np.ones(k)
    levels = np.array([24, -24, 12, -12, 0])
    if k % 512:
        return np.exp2(np.random.permutation(np.resize(levels, k // 32))).repeat(32)
    a = np.empty((k // 512, 16))
    for p in range(k // 512):
        a[p, :8] = np.random.permutation(np.resize(levels, 8))
        for g in range(8):
            far = levels[np.abs(levels - a[p, g]) >= 10]
            a[p, g + 8] = far[np.random.randint(len(far))]
    return np.exp2(a.ravel()).repeat(32)


def f64(x):
    return np.asarray(x).astype(np.float64)


def striped(idx):
    return np.tile(idx.reshape(-1, 16).T, (8, 1)).astype(np.uint16)


def unstriped(offs):
    return offs[:16].T.reshape(-1).astype(np.int64)


E2M1 = np.array([0.0, 0.5, 1.0, 1.5, 2.0, 3.0, 4.0, 6.0, -0.0, -0.5, -1.0, -1.5, -2.0, -3.0, -4.0, -6.0])


def pack_weight(w, fmt):
    k, n = w.shape
    w = f64(np.asarray(w, np.float32).astype(ml_dtypes.bfloat16)).reshape(k // 32, 32, n)
    amax = np.abs(w).max(1)
    if fmt == "e4m3":
        byte = np.frexp(amax)[1] - 1 + 127 - 7
    else:
        mant, ex = np.frexp(amax / 6.0)
        byte = np.where(mant > 0.5, ex, ex - 1) + 127
    byte = np.clip(np.where(amax > 0, byte, 1), 1, 254)
    scaled = (w * np.exp2(127.0 - byte)[:, None, :]).reshape(k, n).astype(np.float32)
    by_word = np.ascontiguousarray(scaled.reshape(k // 512, 128, 4, n).transpose(0, 1, 3, 2))
    if fmt == "e4m3":
        words = by_word.astype(ml_dtypes.float8_e4m3fn).view(np.uint8)
    else:
        c = by_word.astype(ml_dtypes.float4_e2m1fn).view(np.uint8) & 0xF
        words = (c[..., 0::2] | (c[..., 1::2] << 4)).reshape(k // 512, 128, 2 * n)
    return np.ascontiguousarray(words), np.ascontiguousarray(byte.astype(np.uint8).reshape(k // 512, 16, n))


def unpack_weight(words, scales, fmt):
    g, _, n = scales.shape
    words = np.ascontiguousarray(words).reshape(g, 128, n, -1)
    if fmt == "e4m3":
        vals = words.view(ml_dtypes.float8_e4m3fn).astype(np.float64)
    else:
        nib = np.empty((g, 128, n, 4), np.uint8)
        nib[..., 0::2] = words & 0xF
        nib[..., 1::2] = words >> 4
        vals = E2M1[nib]
    vals = vals * np.repeat(np.exp2(scales.astype(np.float64) - 127.0), 8, axis=1)[..., None]
    return vals.transpose(0, 1, 3, 2).reshape(g * 512, n)


def gelu(f):
    return 0.5 * f * (1.0 + np.tanh(np.sqrt(2.0 / np.pi) * (f + 0.044715 * f**3)))


K, R, N, T, J = 512, 1024, 256, 4096, 1024


def setup_inputs():
    n = np.random.standard_normal
    s = mx_kscale(K)[:, None]
    u = mx_kscale(R)[:, None]
    wd = n((R, N)) / np.sqrt(R) / u
    p_tab = pack_weight(n((K, T)) * s, "e4m3")
    p_w1 = pack_weight(n((K, R)) / np.sqrt(3 * K) / s, "e2m1")
    p_w2 = pack_weight(n((K, R)) / np.sqrt(3 * K) / s, "e2m1")
    p_wd8 = pack_weight(wd[:512], "e4m3")
    p_wd4 = pack_weight(wd[512:], "e2m1")
    return {
        "tab_words": p_tab[0],
        "tab_scales": p_tab[1],
        "w0": (n((K, R)) / np.sqrt(3 * K) / s).astype(np.float32),
        "w1_words": p_w1[0],
        "w1_scales": p_w1[1],
        "w2_words": p_w2[0],
        "w2_scales": p_w2[1],
        "sm": (np.random.uniform(0.5, 2.0, R) * u[:, 0]).astype(np.float32),
        "wd8_words": p_wd8[0],
        "wd8_scales": p_wd8[1],
        "wd4_words": p_wd4[0],
        "wd4_scales": p_wd4[1],
        "b": (0.3 * n(N)).astype(np.float32),
        "offs": striped(np.concatenate([np.random.permutation(T)[:J] for _ in range(3)])),
    }


def reference(tab_words, tab_scales, w0, w1_words, w1_scales, w2_words, w2_scales, sm, wd8_words, wd8_scales, wd4_words, wd4_scales, b, offs):
    idx = unstriped(offs).reshape(3, J)
    tab_ = unpack_weight(tab_words, tab_scales, "e4m3")[:, idx]
    w0_ = mxq(f64(w0), 0, "e4m3")
    w1_ = unpack_weight(w1_words, w1_scales, "e2m1")
    w2_ = unpack_weight(w2_words, w2_scales, "e2m1")
    a = w0_.T @ tab_[:, 0] + w1_.T @ tab_[:, 1] + w2_.T @ tab_[:, 2]
    h = f64(sm)[:, None] * gelu(a)
    h_ = mxq(h, 0, "e4m3")
    wd8_ = unpack_weight(wd8_words, wd8_scales, "e4m3")
    wd4_ = unpack_weight(wd4_words, wd4_scales, "e2m1")
    y = wd8_.T @ h_[:512] + wd4_.T @ h_[512:]
    return gelu(y + f64(b)[:, None])

@@ -1,0 +1,224 @@
+from contextlib import ExitStack
+
+import concourse.mybir as mybir
+
+K, R, N, T, J = 512, 1024, 256, 4096, 1024
+FLOPS = 2 * (3 * K * R * J + R * N * J)
+
+F32 = mybir.dt.float32
+BF16 = mybir.dt.bfloat16
+I32 = mybir.dt.int32
+U32 = mybir.dt.uint32
+U16 = mybir.dt.uint16
+U8 = mybir.dt.uint8
+FP8X4 = mybir.dt.float8_e4m3fn_x4
+FP4X4 = mybir.dt.float4_e2m1fn_x4
+GELU = mybir.ActivationFunctionType.Gelu_apprx_tanh
+MULT = mybir.AluOpType.mult
+
+P = 128
+PACK = 4
+HALF = 512
+QUARTER = 256
+
+
+def tile_list_rvq_gelu_mix_gelu_kernel(
+    tc, tab_words, tab_scales, w0, w1_words, w1_scales, w2_words, w2_scales, sm,
+    wd8_words, wd8_scales, wd4_words, wd4_scales, b, offs, out,
+):
+    nc = tc.nc
+    with ExitStack() as ctx:
+        keep = ctx.enter_context(tc.tile_pool(name="keep", bufs=1))
+        psum = ctx.enter_context(tc.psum_pool(name="psum", bufs=1))
+
+        def kept(shape, dtype, name):
+            return keep.tile(shape, dtype, name=name, align_bytes=64)
+
+        offsets = keep.tile([P, 3 * J // 16], U16, name="offsets")
+        nc.sync.dma_start(offsets[:], offs)
+
+        def load_repeated(scales, name):
+            width = scales.shape[2]
+            plane = kept([P, width], U8, name)
+            for q in range(4):
+                rows = scales[0, 4 * q : 4 * q + 4, :].bitcast(I32)
+                nc.sync.dma_start(
+                    plane[32 * q : 32 * q + 32, :].bitcast(I32),
+                    rows.unsqueeze(0).to_broadcast([8, 4, width // 4]),
+                )
+            return plane
+
+        tab_s = load_repeated(tab_scales, "tab_s")
+
+        tab_w = kept([P, T], I32, "tab_w")
+        nc.sync.dma_start(tab_w[:], tab_words[0].rearrange("p t i -> p (t i)").bitcast(I32))
+
+        w_raw, ws_raw = [], []
+        for g, words, scales in ((1, w1_words, w1_scales), (2, w2_words, w2_scales)):
+            raw = kept([P, 2 * R], U8, f"w_raw{g}")
+            nc.sync.dma_start(raw[:].bitcast(I32), words[0].bitcast(I32))
+            w_raw.append(raw)
+            ws_raw.append(load_repeated(scales, f"w{g}_s_raw"))
+
+        w0_rows = w0.rearrange("(p i) r -> p i r", i=PACK)
+        w0_raw = [kept([P, PACK, QUARTER], F32, f"w0_raw{c}") for c in range(4)]
+        for c in range(4):
+            nc.sync.dma_start(w0_raw[c][:], w0_rows[:, :, c * QUARTER : (c + 1) * QUARTER])
+
+        wd8_w = kept([P, N], I32, "wd8_w")
+        nc.sync.dma_start(wd8_w[:], wd8_words[0].rearrange("p n i -> p (n i)").bitcast(I32))
+        wd4_w = kept([P, 2 * N], U8, "wd4_w")
+        nc.sync.dma_start(wd4_w[:].bitcast(I32), wd4_words[0].bitcast(I32))
+        sm_sb = kept([P, 2, PACK], F32, "sm_sb")
+        nc.sync.dma_start(sm_sb[:], sm.rearrange("(u p t) -> p u t", u=2, t=PACK))
+        b_sb = kept([P, 2], F32, "b_sb")
+        with nc.allow_non_contiguous_dma(reason="one bias value to a partition"):
+            nc.sync.dma_start(b_sb[:], b.rearrange("(n p) -> p n", p=P))
+
+        def load_scales(scales, name):
+            plane = kept([P, scales.shape[2]], U8, name)
+            nc.gpsimd.memset(plane[:].bitcast(I32), 0)
+            for q in range(4):
+                nc.gpsimd.dma_start(
+                    plane[32 * q : 32 * q + 4, :].bitcast(I32),
+                    scales[0, 4 * q : 4 * q + 4, :].bitcast(I32),
+                )
+            return plane
+
+        wd8_s = load_scales(wd8_scales, "wd8_s")
+        wd4_s = load_scales(wd4_scales, "wd4_s")
+
+        zero = kept([P, 1], F32, "zero")
+        nc.vector.memset(zero[:], 0.0)
+        no_bias = kept([P, 1], F32, "no_bias")
+        nc.scalar.activation(no_bias[:], zero[:], GELU)
+
+        def offsets_of(g, half):
+            first = (g * J + half * HALF) // 16
+            return offsets[:, first : first + HALF // 16]
+
+        def gather_scales(g, half):
+            picked = keep.tile([P, HALF], U8, name="picked_s", tag=f"picked_s{g}_{half if g == 1 else 0}", align_bytes=64)
+            nc.vector.tensor_copy(picked[:], tab_s[:].indirect(offsets_of(g, half)))
+            return picked
+
+        def gather_words(g, half):
+            picked = kept([P, HALF], U32, f"picked_w{g}_{half}")
+            nc.vector.tensor_copy(picked[:], tab_w[:].bitcast(U32).indirect(offsets_of(g, half)))
+            return picked
+
+        order = (1, 2, 0)
+        v_s = {(g, 0): gather_scales(g, 0) for g in order}
+
+        v_s[1, 1] = gather_scales(1, 1)
+        w_codes, w_scales, v_w = {}, {}, {}
+        for g, raw, raw_s in zip((1, 2), w_raw, ws_raw):
+            v_w[g, 0] = gather_words(g, 0)
+            codes = kept([P, 2 * R], U8, f"w{g}_codes")
+            nc.vector.tensor_copy(
+                codes[:].bitcast(U16).rearrange("p (u t m) -> p u t m", u=2, t=PACK),
+                raw[:].bitcast(U16).rearrange("p (u m t) -> p u t m", u=2, t=PACK),
+            )
+            plane = kept([P, R], U8, f"w{g}_scales")
+            nc.vector.tensor_copy(
+                plane[:].rearrange("p (u t m) -> p u t m", u=2, t=PACK),
+                raw_s[:].rearrange("p (u m t) -> p u t m", u=2, t=PACK),
+            )
+            for u in range(2):
+                for t in range(PACK):
+                    first = u * HALF + t * P
+                    w_codes[g, u, t] = codes[:, 2 * first : 2 * (first + P)].bitcast(FP4X4)
+                    w_scales[g, u, t] = plane[:, first : first + P]
+
+        v_w[0, 0] = gather_words(0, 0)
+
+        for u in range(2):
+            grouped = kept([P, HALF * PACK], BF16, f"w0_grouped{u}")
+            dealt = grouped[:].rearrange("p (a e m i) -> p a m i e", a=2, e=2, i=PACK)
+            for c in range(2):
+                src = w0_raw[2 * u + c][:].rearrange("p i (m a e) -> p a m i e", a=2, e=2)
+                for a in range(2):
+                    nc.scalar.copy(dealt[:, a, c * 64 : (c + 1) * 64], src[:, a])
+            codes = kept([P, HALF], U32, f"w0_codes{u}")
+            plane = kept([P, HALF], U8, f"w0_scales{u}")
+            nc.vector.quantize_mx(codes[:].bitcast(FP8X4), plane[:], grouped[:])
+            for t in range(PACK):
+                w_codes[0, u, t] = codes[:, t * P : (t + 1) * P].bitcast(FP8X4)
+                w_scales[0, u, t] = plane[:, t * P : (t + 1) * P]
+
+        def bank(index, width):
+            tile = psum.tile([P, HALF], F32, name="bank", tag=f"bank{index}")
+            return tile[:, :width]
+
+        def first_layer_pass(acc, g, u, half):
+            for t in range(PACK):
+                nc.tensor.matmul_mx(
+                    acc[t], lhsT=w_codes[g, u, t], lhsT_scale=w_scales[g, u, t],
+                    rhs=v_w[g, half][:].bitcast(FP8X4), rhs_scale=v_s[g, half][:],
+                    start=(g == order[0]), stop=(g == order[-1]),
+                )
+
+        def hidden(acc, u, cols, name):
+            width = cols.stop - cols.start
+            act = kept([P, PACK, width], F32, f"act{name}")
+            for t in range(PACK):
+                nc.scalar.activation(act[:, t, :], acc[t][:, cols], GELU, bias=no_bias[:])
+            grouped = kept([P, width * PACK], BF16, f"h{name}")
+            factor = sm_sb[:, u, :].unsqueeze(1).unsqueeze(3).to_broadcast([P, width // 2, PACK, 2])
+            nc.vector.tensor_tensor(
+                grouped[:].rearrange("p (c e t) -> p c t e", e=2, t=PACK),
+                act[:].rearrange("p t (c e) -> p c t e", e=2),
+                factor,
+                MULT,
+            )
+            codes = kept([P, width], U32, f"h_codes{name}")
+            plane = kept([P, width], U8, f"h_scales{name}")
+            nc.vector.quantize_mx(codes[:].bitcast(FP8X4), plane[:], grouped[:])
+            return codes, plane
+
+        def second_layer(banks, h8, h8_first, h4, width, j_first, name):
+            result = kept([P, 2, width], F32, f"result{name}")
+            step = HALF if width == HALF else P
+            for n in range(2):
+                y = bank(banks[n], width)
+                cols = slice(h8_first, h8_first + width)
+                nc.tensor.matmul_mx(
+                    y, lhsT=wd8_w[:, n * P : (n + 1) * P].bitcast(FP8X4),
+                    lhsT_scale=wd8_s[:, n * P : (n + 1) * P],
+                    rhs=h8[0][:, cols].bitcast(FP8X4), rhs_scale=h8[1][:, cols],
+                    start=True, stop=False,
+                )
+                for c in range(0, width, step):
+                    nc.tensor.matmul_mx(
+                        y[:, c : c + step], lhsT=wd4_w[:, 2 * n * P : 2 * (n + 1) * P].bitcast(FP4X4),
+                        lhsT_scale=wd4_s[:, n * P : (n + 1) * P],
+                        rhs=h4[0][:, c : c + step].bitcast(FP8X4), rhs_scale=h4[1][:, c : c + step],
+                        start=False, stop=(c + step == width),
+                    )
+                nc.scalar.activation(result[:, n, :], y, GELU, bias=b_sb[:, n : n + 1])
+            nc.sync.dma_start(
+                out.rearrange("(n p) j -> p n j", p=P)[:, :, j_first : j_first + width], result[:]
+            )
+
+        whole = slice(0, HALF)
+        acc = [[bank(PACK * u + t, HALF) for t in range(PACK)] for u in range(2)]
+        for g in order:
+            for u in range(2):
+                first_layer_pass(acc[u], g, u, 0)
+
+        for g in order:
+            v_w[g, 1] = gather_words(g, 1)
+        for g in order[1:]:
+            v_s[g, 1] = gather_scales(g, 1)
+
+        h = {(u, 0): hidden(acc[u], u, whole, f"{u}0") for u in range(2)}
+
+        acc = [[bank(PACK * u + t, HALF) for t in range(PACK)] for u in range(2)]
+        for u in range(2):
+            for g in order:
+                first_layer_pass(acc[u], g, u, 1)
+        h[0, 1] = hidden(acc[0], 0, whole, "01")
+        last = [hidden(acc[1], 1, slice(c * QUARTER, (c + 1) * QUARTER), f"11{c}") for c in range(2)]
+        second_layer((0, 1), h[0, 0], 0, h[1, 0], HALF, 0, "0")
+        for c in range(2):
+            second_layer((2 + 2 * c, 3 + 2 * c), h[0, 1], c * QUARTER, last[c], QUARTER, HALF + c * QUARTER, f"1{c}")

@@ -14,6 +14,7 @@ U8 = mybir.dt.uint8
 FP8X4 = mybir.dt.float8_e4m3fn_x4
 FP4X4 = mybir.dt.float4_e2m1fn_x4
 GELU = mybir.ActivationFunctionType.Gelu_apprx_tanh
+COPY = mybir.ActivationFunctionType.Copy
 MULT = mybir.AluOpType.mult
 
 P = 128
@@ -29,6 +30,7 @@ def tile_list_rvq_gelu_mix_gelu_kernel(
     nc = tc.nc
     with ExitStack() as ctx:
         keep = ctx.enter_context(tc.tile_pool(name="keep", bufs=1))
+        reused = ctx.enter_context(tc.tile_pool(name="reused", bufs=1))
         psum = ctx.enter_context(tc.psum_pool(name="psum", bufs=1))
 
         def kept(shape, dtype, name):
@@ -37,56 +39,51 @@ def tile_list_rvq_gelu_mix_gelu_kernel(
         offsets = keep.tile([P, 3 * J // 16], U16, name="offsets")
         nc.sync.dma_start(offsets[:], offs)
 
-        def load_repeated(scales, name):
+        def load_repeated(scales, plane):
             width = scales.shape[2]
-            plane = kept([P, width], U8, name)
             for q in range(4):
                 rows = scales[0, 4 * q : 4 * q + 4, :].bitcast(I32)
                 nc.sync.dma_start(
                     plane[32 * q : 32 * q + 32, :].bitcast(I32),
                     rows.unsqueeze(0).to_broadcast([8, 4, width // 4]),
                 )
-            return plane
 
-        tab_s = load_repeated(tab_scales, "tab_s")
+        tab_s = kept([P, T], U8, "tab_s")
+        load_repeated(tab_scales, tab_s[:])
 
         tab_w = kept([P, T], I32, "tab_w")
         nc.sync.dma_start(tab_w[:], tab_words[0].rearrange("p t i -> p (t i)").bitcast(I32))
 
-        w_raw, ws_raw = [], []
-        for g, words, scales in ((1, w1_words, w1_scales), (2, w2_words, w2_scales)):
-            raw = kept([P, 2 * R], U8, f"w_raw{g}")
-            nc.sync.dma_start(raw[:].bitcast(I32), words[0].bitcast(I32))
-            w_raw.append(raw)
-            ws_raw.append(load_repeated(scales, f"w{g}_s_raw"))
-
+        staged = [keep.tile([P, 3 * R], U8, name="staged", tag=f"staged{g}", align_bytes=64) for g in (1, 2)]
+        w_raw = [tile[:, : 2 * R] for tile in staged]
+        ws_raw = [tile[:, 2 * R :] for tile in staged]
         w0_rows = w0.rearrange("(p i) r -> p i r", i=PACK)
-        w0_raw = [kept([P, PACK, QUARTER], F32, f"w0_raw{c}") for c in range(4)]
-        for c in range(4):
+        w0_raw = [keep.tile([P, PACK, QUARTER], F32, name="w0_raw", tag=f"w0_raw{c}", align_bytes=64) for c in range(4)]
+
+        def load_w0(c):
             nc.sync.dma_start(w0_raw[c][:], w0_rows[:, :, c * QUARTER : (c + 1) * QUARTER])
 
+        nc.sync.dma_start(w_raw[0].bitcast(I32), w1_words[0].bitcast(I32))
+        load_repeated(w1_scales, ws_raw[0])
+        nc.sync.dma_start(w_raw[1].bitcast(I32), w2_words[0].bitcast(I32))
+        load_w0(0)
+        load_repeated(w2_scales, ws_raw[1])
+        for c in range(1, 4):
+            load_w0(c)
+
+        sm_sb = kept([P, 2, PACK], F32, "sm_sb")
+        nc.sync.dma_start(sm_sb[:], sm.rearrange("(u p t) -> p u t", u=2, t=PACK))
         wd8_w = kept([P, N], I32, "wd8_w")
         nc.sync.dma_start(wd8_w[:], wd8_words[0].rearrange("p n i -> p (n i)").bitcast(I32))
         wd4_w = kept([P, 2 * N], U8, "wd4_w")
         nc.sync.dma_start(wd4_w[:].bitcast(I32), wd4_words[0].bitcast(I32))
-        sm_sb = kept([P, 2, PACK], F32, "sm_sb")
-        nc.sync.dma_start(sm_sb[:], sm.rearrange("(u p t) -> p u t", u=2, t=PACK))
+        wd8_s = kept([P, N], U8, "wd8_s")
+        load_repeated(wd8_scales, wd8_s[:])
+        wd4_s = kept([P, N], U8, "wd4_s")
+        load_repeated(wd4_scales, wd4_s[:])
         b_sb = kept([P, 2], F32, "b_sb")
         with nc.allow_non_contiguous_dma(reason="one bias value to a partition"):
             nc.sync.dma_start(b_sb[:], b.rearrange("(n p) -> p n", p=P))
-
-        def load_scales(scales, name):
-            plane = kept([P, scales.shape[2]], U8, name)
-            nc.gpsimd.memset(plane[:].bitcast(I32), 0)
-            for q in range(4):
-                nc.gpsimd.dma_start(
-                    plane[32 * q : 32 * q + 4, :].bitcast(I32),
-                    scales[0, 4 * q : 4 * q + 4, :].bitcast(I32),
-                )
-            return plane
-
-        wd8_s = load_scales(wd8_scales, "wd8_s")
-        wd4_s = load_scales(wd4_scales, "wd4_s")
 
         zero = kept([P, 1], F32, "zero")
         nc.vector.memset(zero[:], 0.0)
@@ -97,13 +94,20 @@ def tile_list_rvq_gelu_mix_gelu_kernel(
             first = (g * J + half * HALF) // 16
             return offsets[:, first : first + HALF // 16]
 
+        late_words = {2: 0, 0: 4 * HALF}
+
         def gather_scales(g, half):
-            picked = keep.tile([P, HALF], U8, name="picked_s", tag=f"picked_s{g}_{half if g == 1 else 0}", align_bytes=64)
+            tag = {(2, 1): "picked_s0_0", (0, 1): "staged2"}.get((g, half), f"picked_s{g}_{half}")
+            picked = keep.tile([P, HALF], U8, name="picked_s", tag=tag, align_bytes=64)
             nc.vector.tensor_copy(picked[:], tab_s[:].indirect(offsets_of(g, half)))
             return picked
 
         def gather_words(g, half):
-            picked = kept([P, HALF], U32, f"picked_w{g}_{half}")
+            if half == 1 and g in late_words:
+                picked = reused.tile([P, HALF], U32, name=f"late_w{g}", offset=late_words[g], align_bytes=64)
+            else:
+                tag = {(1, 0): "picked_w1", (2, 0): "staged1", (0, 0): "staged2", (1, 1): "w0_grouped0"}[g, half]
+                picked = keep.tile([P, HALF], U32, name="picked_w", tag=tag, align_bytes=64)
             nc.vector.tensor_copy(picked[:], tab_w[:].bitcast(U32).indirect(offsets_of(g, half)))
             return picked
 
@@ -117,12 +121,12 @@ def tile_list_rvq_gelu_mix_gelu_kernel(
             codes = kept([P, 2 * R], U8, f"w{g}_codes")
             nc.vector.tensor_copy(
                 codes[:].bitcast(U16).rearrange("p (u t m) -> p u t m", u=2, t=PACK),
-                raw[:].bitcast(U16).rearrange("p (u m t) -> p u t m", u=2, t=PACK),
+                raw.bitcast(U16).rearrange("p (u m t) -> p u t m", u=2, t=PACK),
             )
             plane = kept([P, R], U8, f"w{g}_scales")
             nc.vector.tensor_copy(
                 plane[:].rearrange("p (u t m) -> p u t m", u=2, t=PACK),
-                raw_s[:].rearrange("p (u m t) -> p u t m", u=2, t=PACK),
+                raw_s.rearrange("p (u m t) -> p u t m", u=2, t=PACK),
             )
             for u in range(2):
                 for t in range(PACK):
@@ -133,7 +137,10 @@ def tile_list_rvq_gelu_mix_gelu_kernel(
         v_w[0, 0] = gather_words(0, 0)
 
         for u in range(2):
-            grouped = kept([P, HALF * PACK], BF16, f"w0_grouped{u}")
+            if u == 0:
+                grouped = kept([P, HALF * PACK], BF16, "w0_grouped0")
+            else:
+                grouped = reused.tile([P, HALF * PACK], BF16, name="w0_grouped1", offset=0, align_bytes=64)
             dealt = grouped[:].rearrange("p (a e m i) -> p a m i e", a=2, e=2, i=PACK)
             for c in range(2):
                 src = w0_raw[2 * u + c][:].rearrange("p i (m a e) -> p a m i e", a=2, e=2)
@@ -158,30 +165,55 @@ def tile_list_rvq_gelu_mix_gelu_kernel(
                     start=(g == order[0]), stop=(g == order[-1]),
                 )
 
-        def hidden(acc, u, cols, name):
-            width = cols.stop - cols.start
-            act = kept([P, PACK, width], F32, f"act{name}")
+        def activate(acc, tag):
+            act = keep.tile([P, PACK, HALF], F32, name="act", tag=tag, align_bytes=64)
             for t in range(PACK):
-                nc.scalar.activation(act[:, t, :], acc[t][:, cols], GELU, bias=no_bias[:])
-            grouped = kept([P, width * PACK], BF16, f"h{name}")
+                nc.scalar.activation(act[:, t, :], acc[t], GELU, bias=no_bias[:])
+            return act
+
+        def smooth_on_vector(grouped, act, u):
+            width = act.shape[2]
             factor = sm_sb[:, u, :].unsqueeze(1).unsqueeze(3).to_broadcast([P, width // 2, PACK, 2])
             nc.vector.tensor_tensor(
-                grouped[:].rearrange("p (c e t) -> p c t e", e=2, t=PACK),
-                act[:].rearrange("p t (c e) -> p c t e", e=2),
+                grouped.rearrange("p (c e t) -> p c t e", e=2, t=PACK),
+                act.rearrange("p t (c e) -> p c t e", e=2),
                 factor,
                 MULT,
             )
-            codes = kept([P, width], U32, f"h_codes{name}")
-            plane = kept([P, width], U8, f"h_scales{name}")
-            nc.vector.quantize_mx(codes[:].bitcast(FP8X4), plane[:], grouped[:])
-            return codes, plane
 
-        def second_layer(banks, h8, h8_first, h4, width, j_first, name):
+        def smooth_on_scalar(grouped, act, u):
+            rows = kept([P, PACK, HALF], BF16, "smoothed")
+            for t in range(PACK):
+                nc.scalar.activation(rows[:, t, :], act[:, t, :], COPY, scale=sm_sb[:, u, t : t + 1])
+            nc.vector.tensor_copy(
+                grouped.rearrange("p (c e t) -> p c t e", e=PACK, t=PACK),
+                rows[:].rearrange("p t (c e) -> p c t e", e=PACK),
+            )
+
+        def hidden_in_pieces(act, u, widths, name):
+            codes = kept([P, HALF], U32, f"h_codes{name}")
+            plane = kept([P, HALF], U8, f"h_scales{name}")
+            pieces = [slice(sum(widths[:c]), sum(widths[: c + 1])) for c in range(len(widths))]
+            grouped = [kept([P, w * PACK], BF16, f"h{name}{c}") for c, w in enumerate(widths)]
+
+            def quantise(c):
+                nc.vector.quantize_mx(codes[:, pieces[c]].bitcast(FP8X4), plane[:, pieces[c]], grouped[c][:])
+
+            for c, cols in enumerate(pieces):
+                smooth_on_vector(grouped[c][:], act[:, :, cols], u)
+                if c > 0:
+                    quantise(c - 1)
+            quantise(len(pieces) - 1)
+            return codes[:], plane[:], pieces
+
+        out_rows = out.rearrange("(n p) j -> p n j", p=P)
+
+        def second_layer(banks, h8, h4, cols, j_first, name):
+            width = cols.stop - cols.start
             result = kept([P, 2, width], F32, f"result{name}")
             step = HALF if width == HALF else P
             for n in range(2):
                 y = bank(banks[n], width)
-                cols = slice(h8_first, h8_first + width)
                 nc.tensor.matmul_mx(
                     y, lhsT=wd8_w[:, n * P : (n + 1) * P].bitcast(FP8X4),
                     lhsT_scale=wd8_s[:, n * P : (n + 1) * P],
@@ -189,36 +221,42 @@ def tile_list_rvq_gelu_mix_gelu_kernel(
                     start=True, stop=False,
                 )
                 for c in range(0, width, step):
+                    part = slice(cols.start + c, cols.start + c + step)
                     nc.tensor.matmul_mx(
                         y[:, c : c + step], lhsT=wd4_w[:, 2 * n * P : 2 * (n + 1) * P].bitcast(FP4X4),
                         lhsT_scale=wd4_s[:, n * P : (n + 1) * P],
-                        rhs=h4[0][:, c : c + step].bitcast(FP8X4), rhs_scale=h4[1][:, c : c + step],
+                        rhs=h4[0][:, part].bitcast(FP8X4), rhs_scale=h4[1][:, part],
                         start=False, stop=(c + step == width),
                     )
                 nc.scalar.activation(result[:, n, :], y, GELU, bias=b_sb[:, n : n + 1])
-            nc.sync.dma_start(
-                out.rearrange("(n p) j -> p n j", p=P)[:, :, j_first : j_first + width], result[:]
-            )
+            nc.sync.dma_start(out_rows[:, :, j_first + cols.start : j_first + cols.stop], result[:])
 
-        whole = slice(0, HALF)
         acc = [[bank(PACK * u + t, HALF) for t in range(PACK)] for u in range(2)]
-        for g in order:
-            for u in range(2):
-                first_layer_pass(acc[u], g, u, 0)
+        for g, u in ((1, 0), (1, 1), (2, 0), (0, 0), (2, 1), (0, 1)):
+            first_layer_pass(acc[u], g, u, 0)
 
         for g in order:
             v_w[g, 1] = gather_words(g, 1)
         for g in order[1:]:
             v_s[g, 1] = gather_scales(g, 1)
 
-        h = {(u, 0): hidden(acc[u], u, whole, f"{u}0") for u in range(2)}
+        act0 = activate(acc[0], "w0_raw3")
+        act1 = activate(acc[1], "act10")
+        grouped = keep.tile([P, 2 * HALF * PACK], BF16, name="h0", tag="tab_s", align_bytes=64)
+        smooth_on_vector(grouped[:, : HALF * PACK], act0[:], 0)
+        smooth_on_scalar(grouped[:, HALF * PACK :], act1[:], 1)
+        codes = kept([P, 2 * HALF], U32, "h_codes0")
+        plane = kept([P, 2 * HALF], U8, "h_scales0")
+        nc.vector.quantize_mx(codes[:].bitcast(FP8X4), plane[:], grouped[:])
+        h_first = [(codes[:, u * HALF : (u + 1) * HALF], plane[:, u * HALF : (u + 1) * HALF]) for u in range(2)]
 
         acc = [[bank(PACK * u + t, HALF) for t in range(PACK)] for u in range(2)]
-        for u in range(2):
-            for g in order:
-                first_layer_pass(acc[u], g, u, 1)
-        h[0, 1] = hidden(acc[0], 0, whole, "01")
-        last = [hidden(acc[1], 1, slice(c * QUARTER, (c + 1) * QUARTER), f"11{c}") for c in range(2)]
-        second_layer((0, 1), h[0, 0], 0, h[1, 0], HALF, 0, "0")
-        for c in range(2):
-            second_layer((2 + 2 * c, 3 + 2 * c), h[0, 1], c * QUARTER, last[c], QUARTER, HALF + c * QUARTER, f"1{c}")
+        for g, u in ((1, 0), (2, 0), (1, 1), (0, 0), (2, 1), (0, 1)):
+            first_layer_pass(acc[u], g, u, 1)
+        act0 = activate(acc[0], "act01")
+        act1 = activate(acc[1], "act11")
+        h8 = hidden_in_pieces(act0[:], 0, [QUARTER, QUARTER], "01")
+        h4 = hidden_in_pieces(act1[:], 1, [QUARTER, P, P], "11")
+        second_layer((0, 1), h_first[0], h_first[1], slice(0, HALF), 0, "0")
+        for c, cols in enumerate(h4[2]):
+            second_layer((2 + 2 * c, 3 + 2 * c), h8, h4, cols, HALF, f"1{c}")

@@ -36,51 +36,51 @@ def tile_list_rvq_gelu_mix_gelu_kernel(
         def kept(shape, dtype, name):
             return keep.tile(shape, dtype, name=name, align_bytes=64)
 
+        def placed(shape, dtype, name, offset):
+            return reused.tile(shape, dtype, name=name, offset=offset, align_bytes=64)
+
         offsets = keep.tile([P, 3 * J // 16], U16, name="offsets")
         nc.sync.dma_start(offsets[:], offs)
 
-        def load_repeated(scales, plane):
-            width = scales.shape[2]
+        def load_scale_rows(scales, plane):
             for q in range(4):
-                rows = scales[0, 4 * q : 4 * q + 4, :].bitcast(I32)
                 nc.sync.dma_start(
-                    plane[32 * q : 32 * q + 32, :].bitcast(I32),
-                    rows.unsqueeze(0).to_broadcast([8, 4, width // 4]),
+                    plane[32 * q : 32 * q + 4, :].bitcast(I32), scales[0, 4 * q : 4 * q + 4, :].bitcast(I32)
                 )
 
         tab_s = kept([P, T], U8, "tab_s")
-        load_repeated(tab_scales, tab_s[:])
+        nc.vector.memset(tab_s[:].bitcast(I32), 0)
+        load_scale_rows(tab_scales, tab_s[:])
 
+        w_raw = [kept([P, 2 * R], U8, f"w{g}_raw") for g in (1, 2)]
+        ws_raw = [placed([P, R], U8, "w1_s_raw", 3 * HALF), kept([P, R], U8, "w2_s_raw")]
+        wd8_s = kept([P, N], U8, "wd8_s")
+        wd4_s = kept([P, N], U8, "wd4_s")
+        for plane in ws_raw + [wd8_s, wd4_s]:
+            nc.vector.memset(plane[:].bitcast(I32), 0)
+
+        for raw, words in zip(w_raw, (w1_words, w2_words)):
+            nc.sync.dma_start(raw[:].bitcast(I32), words[0].bitcast(I32))
         tab_w = kept([P, T], I32, "tab_w")
         nc.sync.dma_start(tab_w[:], tab_words[0].rearrange("p t i -> p (t i)").bitcast(I32))
+        load_scale_rows(w1_scales, ws_raw[0][:])
 
-        staged = [keep.tile([P, 3 * R], U8, name="staged", tag=f"staged{g}", align_bytes=64) for g in (1, 2)]
-        w_raw = [tile[:, : 2 * R] for tile in staged]
-        ws_raw = [tile[:, 2 * R :] for tile in staged]
         w0_rows = w0.rearrange("(p i) r -> p i r", i=PACK)
-        w0_raw = [keep.tile([P, PACK, QUARTER], F32, name="w0_raw", tag=f"w0_raw{c}", align_bytes=64) for c in range(4)]
-
-        def load_w0(c):
+        w0_raw = [kept([P, PACK, QUARTER], F32, f"w0_raw{c}") for c in range(3)]
+        w0_raw.append(placed([P, PACK, QUARTER], F32, "w0_raw3", 8 * HALF))
+        for c in range(4):
             nc.sync.dma_start(w0_raw[c][:], w0_rows[:, :, c * QUARTER : (c + 1) * QUARTER])
-
-        nc.sync.dma_start(w_raw[0].bitcast(I32), w1_words[0].bitcast(I32))
-        load_repeated(w1_scales, ws_raw[0])
-        nc.sync.dma_start(w_raw[1].bitcast(I32), w2_words[0].bitcast(I32))
-        load_w0(0)
-        load_repeated(w2_scales, ws_raw[1])
-        for c in range(1, 4):
-            load_w0(c)
-
+            if c == 1:
+                load_scale_rows(w2_scales, ws_raw[1][:])
         sm_sb = kept([P, 2, PACK], F32, "sm_sb")
         nc.sync.dma_start(sm_sb[:], sm.rearrange("(u p t) -> p u t", u=2, t=PACK))
+
         wd8_w = kept([P, N], I32, "wd8_w")
         nc.sync.dma_start(wd8_w[:], wd8_words[0].rearrange("p n i -> p (n i)").bitcast(I32))
         wd4_w = kept([P, 2 * N], U8, "wd4_w")
         nc.sync.dma_start(wd4_w[:].bitcast(I32), wd4_words[0].bitcast(I32))
-        wd8_s = kept([P, N], U8, "wd8_s")
-        load_repeated(wd8_scales, wd8_s[:])
-        wd4_s = kept([P, N], U8, "wd4_s")
-        load_repeated(wd4_scales, wd4_s[:])
+        load_scale_rows(wd8_scales, wd8_s[:])
+        load_scale_rows(wd4_scales, wd4_s[:])
         b_sb = kept([P, 2], F32, "b_sb")
         with nc.allow_non_contiguous_dma(reason="one bias value to a partition"):
             nc.sync.dma_start(b_sb[:], b.rearrange("(n p) -> p n", p=P))
@@ -94,20 +94,23 @@ def tile_list_rvq_gelu_mix_gelu_kernel(
             first = (g * J + half * HALF) // 16
             return offsets[:, first : first + HALF // 16]
 
-        late_words = {2: 0, 0: 4 * HALF}
-
         def gather_scales(g, half):
-            tag = {(2, 1): "picked_s0_0", (0, 1): "staged2"}.get((g, half), f"picked_s{g}_{half}")
-            picked = keep.tile([P, HALF], U8, name="picked_s", tag=tag, align_bytes=64)
+            if (g, half) == (2, 1):
+                picked = placed([P, HALF], U8, "picked_s2_1", 8 * HALF)
+            else:
+                tag = "picked_s0_0" if g == 0 else f"picked_s{g}_{half}"
+                picked = keep.tile([P, HALF], U8, name="picked_s", tag=tag, align_bytes=64)
             nc.vector.tensor_copy(picked[:], tab_s[:].indirect(offsets_of(g, half)))
             return picked
 
+        word_places = {(2, 0): 0, (0, 0): 4 * HALF, (0, 1): 9 * HALF}
+        word_tags = {(1, 0): "picked_w1_0", (1, 1): "w0_raw1", (2, 1): "w0_raw2"}
+
         def gather_words(g, half):
-            if half == 1 and g in late_words:
-                picked = reused.tile([P, HALF], U32, name=f"late_w{g}", offset=late_words[g], align_bytes=64)
+            if (g, half) in word_places:
+                picked = placed([P, HALF], U32, f"picked_w{g}_{half}", word_places[g, half])
             else:
-                tag = {(1, 0): "picked_w1", (2, 0): "staged1", (0, 0): "staged2", (1, 1): "w0_grouped0"}[g, half]
-                picked = keep.tile([P, HALF], U32, name="picked_w", tag=tag, align_bytes=64)
+                picked = keep.tile([P, HALF], U32, name="picked_w", tag=word_tags[g, half], align_bytes=64)
             nc.vector.tensor_copy(picked[:], tab_w[:].bitcast(U32).indirect(offsets_of(g, half)))
             return picked
 
@@ -117,16 +120,15 @@ def tile_list_rvq_gelu_mix_gelu_kernel(
         v_s[1, 1] = gather_scales(1, 1)
         w_codes, w_scales, v_w = {}, {}, {}
         for g, raw, raw_s in zip((1, 2), w_raw, ws_raw):
-            v_w[g, 0] = gather_words(g, 0)
             codes = kept([P, 2 * R], U8, f"w{g}_codes")
             nc.vector.tensor_copy(
                 codes[:].bitcast(U16).rearrange("p (u t m) -> p u t m", u=2, t=PACK),
-                raw.bitcast(U16).rearrange("p (u m t) -> p u t m", u=2, t=PACK),
+                raw[:].bitcast(U16).rearrange("p (u m t) -> p u t m", u=2, t=PACK),
             )
             plane = kept([P, R], U8, f"w{g}_scales")
             nc.vector.tensor_copy(
                 plane[:].rearrange("p (u t m) -> p u t m", u=2, t=PACK),
-                raw_s.rearrange("p (u m t) -> p u t m", u=2, t=PACK),
+                raw_s[:].rearrange("p (u m t) -> p u t m", u=2, t=PACK),
             )
             for u in range(2):
                 for t in range(PACK):
@@ -134,13 +136,11 @@ def tile_list_rvq_gelu_mix_gelu_kernel(
                     w_codes[g, u, t] = codes[:, 2 * first : 2 * (first + P)].bitcast(FP4X4)
                     w_scales[g, u, t] = plane[:, first : first + P]
 
-        v_w[0, 0] = gather_words(0, 0)
+        for g in order:
+            v_w[g, 0] = gather_words(g, 0)
 
         for u in range(2):
-            if u == 0:
-                grouped = kept([P, HALF * PACK], BF16, "w0_grouped0")
-            else:
-                grouped = reused.tile([P, HALF * PACK], BF16, name="w0_grouped1", offset=0, align_bytes=64)
+            grouped = kept([P, HALF * PACK], BF16, f"w0_grouped{u}")
             dealt = grouped[:].rearrange("p (a e m i) -> p a m i e", a=2, e=2, i=PACK)
             for c in range(2):
                 src = w0_raw[2 * u + c][:].rearrange("p i (m a e) -> p a m i e", a=2, e=2)
@@ -165,8 +165,7 @@ def tile_list_rvq_gelu_mix_gelu_kernel(
                     start=(g == order[0]), stop=(g == order[-1]),
                 )
 
-        def activate(acc, tag):
-            act = keep.tile([P, PACK, HALF], F32, name="act", tag=tag, align_bytes=64)
+        def activate(acc, act):
             for t in range(PACK):
                 nc.scalar.activation(act[:, t, :], acc[t], GELU, bias=no_bias[:])
             return act
@@ -181,16 +180,19 @@ def tile_list_rvq_gelu_mix_gelu_kernel(
                 MULT,
             )
 
-        def smooth_on_scalar(grouped, act, u):
-            rows = kept([P, PACK, HALF], BF16, "smoothed")
+        def smooth_rows(act, u, name):
+            rows = kept([P, PACK, act.shape[2]], BF16, name)
             for t in range(PACK):
                 nc.scalar.activation(rows[:, t, :], act[:, t, :], COPY, scale=sm_sb[:, u, t : t + 1])
+            return rows
+
+        def interleave(grouped, rows):
             nc.vector.tensor_copy(
                 grouped.rearrange("p (c e t) -> p c t e", e=PACK, t=PACK),
-                rows[:].rearrange("p t (c e) -> p c t e", e=PACK),
+                rows.rearrange("p t (c e) -> p c t e", e=PACK),
             )
 
-        def hidden_in_pieces(act, u, widths, name):
+        def quantise_in_pieces(fill, widths, name):
             codes = kept([P, HALF], U32, f"h_codes{name}")
             plane = kept([P, HALF], U8, f"h_scales{name}")
             pieces = [slice(sum(widths[:c]), sum(widths[: c + 1])) for c in range(len(widths))]
@@ -200,7 +202,7 @@ def tile_list_rvq_gelu_mix_gelu_kernel(
                 nc.vector.quantize_mx(codes[:, pieces[c]].bitcast(FP8X4), plane[:, pieces[c]], grouped[c][:])
 
             for c, cols in enumerate(pieces):
-                smooth_on_vector(grouped[c][:], act[:, :, cols], u)
+                fill(grouped[c][:], cols)
                 if c > 0:
                     quantise(c - 1)
             quantise(len(pieces) - 1)
@@ -235,16 +237,17 @@ def tile_list_rvq_gelu_mix_gelu_kernel(
         for g, u in ((1, 0), (1, 1), (2, 0), (0, 0), (2, 1), (0, 1)):
             first_layer_pass(acc[u], g, u, 0)
 
-        for g in order:
-            v_w[g, 1] = gather_words(g, 1)
-        for g in order[1:]:
-            v_s[g, 1] = gather_scales(g, 1)
+        v_w[1, 1] = gather_words(1, 1)
+        v_w[2, 1] = gather_words(2, 1)
+        v_s[2, 1] = gather_scales(2, 1)
+        v_w[0, 1] = gather_words(0, 1)
+        v_s[0, 1] = gather_scales(0, 1)
 
-        act0 = activate(acc[0], "w0_raw3")
-        act1 = activate(acc[1], "act10")
+        act0 = activate(acc[0], placed([P, PACK, HALF], F32, "act00", 13 * HALF))
+        act1 = activate(acc[1], kept([P, PACK, HALF], F32, "act10"))
         grouped = keep.tile([P, 2 * HALF * PACK], BF16, name="h0", tag="tab_s", align_bytes=64)
         smooth_on_vector(grouped[:, : HALF * PACK], act0[:], 0)
-        smooth_on_scalar(grouped[:, HALF * PACK :], act1[:], 1)
+        interleave(grouped[:, HALF * PACK :], smooth_rows(act1[:], 1, "smoothed0")[:])
         codes = kept([P, 2 * HALF], U32, "h_codes0")
         plane = kept([P, 2 * HALF], U8, "h_scales0")
         nc.vector.quantize_mx(codes[:].bitcast(FP8X4), plane[:], grouped[:])
@@ -253,10 +256,18 @@ def tile_list_rvq_gelu_mix_gelu_kernel(
         acc = [[bank(PACK * u + t, HALF) for t in range(PACK)] for u in range(2)]
         for g, u in ((1, 0), (2, 0), (1, 1), (0, 0), (2, 1), (0, 1)):
             first_layer_pass(acc[u], g, u, 1)
-        act0 = activate(acc[0], "act01")
-        act1 = activate(acc[1], "act11")
-        h8 = hidden_in_pieces(act0[:], 0, [QUARTER, QUARTER], "01")
-        h4 = hidden_in_pieces(act1[:], 1, [QUARTER, P, P], "11")
+        act0 = activate(acc[0], kept([P, PACK, HALF], F32, "act01"))
+        act1 = activate(acc[1], kept([P, PACK, HALF], F32, "act11"))
+        rows = smooth_rows(act1[:, :, :QUARTER], 1, "smoothed1")
+
+        def fill_last(grouped, cols):
+            if cols.start == 0:
+                interleave(grouped, rows[:])
+            else:
+                smooth_on_vector(grouped, act1[:, :, cols], 1)
+
+        h8 = quantise_in_pieces(lambda grouped, cols: smooth_on_vector(grouped, act0[:, :, cols], 0), [QUARTER, QUARTER], "01")
+        h4 = quantise_in_pieces(fill_last, [QUARTER, P, P], "11")
         second_layer((0, 1), h_first[0], h_first[1], slice(0, HALF), 0, "0")
         for c, cols in enumerate(h4[2]):
             second_layer((2 + 2 * c, 3 + 2 * c), h8, h4, cols, HALF, f"1{c}")

@@ -16,6 +16,7 @@ FP4X4 = mybir.dt.float4_e2m1fn_x4
 GELU = mybir.ActivationFunctionType.Gelu_apprx_tanh
 COPY = mybir.ActivationFunctionType.Copy
 MULT = mybir.AluOpType.mult
+ADD = mybir.AluOpType.add
 
 P = 128
 PACK = 4
@@ -66,8 +67,12 @@ def tile_list_rvq_gelu_mix_gelu_kernel(
         load_scale_rows(w1_scales, ws_raw[0][:])
 
         w0_rows = w0.rearrange("(p i) r -> p i r", i=PACK)
-        w0_raw = [kept([P, PACK, QUARTER], F32, f"w0_raw{c}") for c in range(3)]
-        w0_raw.append(placed([P, PACK, QUARTER], F32, "w0_raw3", 8 * HALF))
+        w0_raw = [
+            kept([P, PACK, QUARTER], F32, "w0_raw0"),
+            placed([P, PACK, QUARTER], F32, "w0_raw1", 32 * HALF),
+            kept([P, PACK, QUARTER], F32, "w0_raw2"),
+            placed([P, PACK, QUARTER], F32, "w0_raw3", 8 * HALF),
+        ]
         for c in range(4):
             nc.sync.dma_start(w0_raw[c][:], w0_rows[:, :, c * QUARTER : (c + 1) * QUARTER])
             if c == 1:
@@ -87,7 +92,7 @@ def tile_list_rvq_gelu_mix_gelu_kernel(
 
         zero = kept([P, 1], F32, "zero")
         nc.vector.memset(zero[:], 0.0)
-        no_bias = kept([P, 1], F32, "no_bias")
+        no_bias = keep.tile([P, 1], F32, name="no_bias", tag="no_bias", align_bytes=64)
         nc.scalar.activation(no_bias[:], zero[:], GELU)
 
         def offsets_of(g, half):
@@ -98,13 +103,13 @@ def tile_list_rvq_gelu_mix_gelu_kernel(
             if (g, half) == (2, 1):
                 picked = placed([P, HALF], U8, "picked_s2_1", 8 * HALF)
             else:
-                tag = "picked_s0_0" if g == 0 else f"picked_s{g}_{half}"
+                tag = "no_bias" if (g, half) == (0, 1) else f"picked_s{g}_{half}"
                 picked = keep.tile([P, HALF], U8, name="picked_s", tag=tag, align_bytes=64)
             nc.vector.tensor_copy(picked[:], tab_s[:].indirect(offsets_of(g, half)))
             return picked
 
-        word_places = {(2, 0): 0, (0, 0): 4 * HALF, (0, 1): 9 * HALF}
-        word_tags = {(1, 0): "picked_w1_0", (1, 1): "w0_raw1", (2, 1): "w0_raw2"}
+        word_places = {(2, 0): 0, (0, 0): 4 * HALF, (1, 1): 33 * HALF, (0, 1): 9 * HALF}
+        word_tags = {(1, 0): "picked_w1_0", (2, 1): "w0_raw2"}
 
         def gather_words(g, half):
             if (g, half) in word_places:
@@ -119,27 +124,29 @@ def tile_list_rvq_gelu_mix_gelu_kernel(
 
         v_s[1, 1] = gather_scales(1, 1)
         w_codes, w_scales, v_w = {}, {}, {}
-        for g, raw, raw_s in zip((1, 2), w_raw, ws_raw):
+        for g, raw in zip((1, 2), w_raw):
             codes = kept([P, 2 * R], U8, f"w{g}_codes")
             nc.vector.tensor_copy(
                 codes[:].bitcast(U16).rearrange("p (u t m) -> p u t m", u=2, t=PACK),
                 raw[:].bitcast(U16).rearrange("p (u m t) -> p u t m", u=2, t=PACK),
             )
-            plane = kept([P, R], U8, f"w{g}_scales")
-            nc.vector.tensor_copy(
-                plane[:].rearrange("p (u t m) -> p u t m", u=2, t=PACK),
-                raw_s[:].rearrange("p (u m t) -> p u t m", u=2, t=PACK),
-            )
             for u in range(2):
                 for t in range(PACK):
                     first = u * HALF + t * P
                     w_codes[g, u, t] = codes[:, 2 * first : 2 * (first + P)].bitcast(FP4X4)
+
+        def deal_scales(g, units, plane):
+            raw_s = ws_raw[g - 1][:, units[0] * HALF : (units[-1] + 1) * HALF]
+            nc.vector.tensor_copy(
+                plane[:].rearrange("p (u t m) -> p u t m", t=PACK, m=P),
+                raw_s.rearrange("p (u m t) -> p u t m", t=PACK, m=P),
+            )
+            for i, u in enumerate(units):
+                for t in range(PACK):
+                    first = i * HALF + t * P
                     w_scales[g, u, t] = plane[:, first : first + P]
 
-        for g in order:
-            v_w[g, 0] = gather_words(g, 0)
-
-        for u in range(2):
+        def quantise_w0(u):
             grouped = kept([P, HALF * PACK], BF16, f"w0_grouped{u}")
             dealt = grouped[:].rearrange("p (a e m i) -> p a m i e", a=2, e=2, i=PACK)
             for c in range(2):
@@ -153,6 +160,14 @@ def tile_list_rvq_gelu_mix_gelu_kernel(
                 w_codes[0, u, t] = codes[:, t * P : (t + 1) * P].bitcast(FP8X4)
                 w_scales[0, u, t] = plane[:, t * P : (t + 1) * P]
 
+        deal_scales(1, (0, 1), kept([P, R], U8, "w1_scales"))
+        deal_scales(2, (0,), kept([P, HALF], U8, "w2_scales0"))
+        for g in order:
+            v_w[g, 0] = gather_words(g, 0)
+        quantise_w0(0)
+        deal_scales(2, (1,), placed([P, HALF], U8, "w2_scales1", 32 * HALF))
+        quantise_w0(1)
+
         def bank(index, width):
             tile = psum.tile([P, HALF], F32, name="bank", tag=f"bank{index}")
             return tile[:, :width]
@@ -165,9 +180,9 @@ def tile_list_rvq_gelu_mix_gelu_kernel(
                     start=(g == order[0]), stop=(g == order[-1]),
                 )
 
-        def activate(acc, act):
+        def activate(acc, act, with_bias_tile=0):
             for t in range(PACK):
-                nc.scalar.activation(act[:, t, :], acc[t], GELU, bias=no_bias[:])
+                nc.scalar.activation(act[:, t, :], acc[t], GELU, bias=no_bias[:] if t < with_bias_tile else 0.0)
             return act
 
         def smooth_on_vector(grouped, act, u):
@@ -184,6 +199,12 @@ def tile_list_rvq_gelu_mix_gelu_kernel(
             rows = kept([P, PACK, act.shape[2]], BF16, name)
             for t in range(PACK):
                 nc.scalar.activation(rows[:, t, :], act[:, t, :], COPY, scale=sm_sb[:, u, t : t + 1])
+            return rows
+
+        def smooth_rows_on_gpsimd(act, u, name):
+            rows = kept([P, PACK, act.shape[2]], BF16, name)
+            for t in range(PACK):
+                nc.gpsimd.tensor_scalar(rows[:, t, :], act[:, t, :], sm_sb[:, u, t : t + 1], 0.0, MULT, ADD)
             return rows
 
         def interleave(grouped, rows):
@@ -208,11 +229,8 @@ def tile_list_rvq_gelu_mix_gelu_kernel(
             quantise(len(pieces) - 1)
             return codes[:], plane[:], pieces
 
-        out_rows = out.rearrange("(n p) j -> p n j", p=P)
-
         def second_layer(banks, h8, h4, cols, j_first, name):
             width = cols.stop - cols.start
-            result = kept([P, 2, width], F32, f"result{name}")
             step = HALF if width == HALF else P
             for n in range(2):
                 y = bank(banks[n], width)
@@ -230,8 +248,9 @@ def tile_list_rvq_gelu_mix_gelu_kernel(
                         rhs=h4[0][:, part].bitcast(FP8X4), rhs_scale=h4[1][:, part],
                         start=False, stop=(c + step == width),
                     )
-                nc.scalar.activation(result[:, n, :], y, GELU, bias=b_sb[:, n : n + 1])
-            nc.sync.dma_start(out_rows[:, :, j_first + cols.start : j_first + cols.stop], result[:])
+                result = kept([P, width], F32, f"result{name}_{n}")
+                nc.scalar.activation(result[:], y, GELU, bias=b_sb[:, n : n + 1])
+                nc.sync.dma_start(out[n * P : (n + 1) * P, j_first + cols.start : j_first + cols.stop], result[:])
 
         acc = [[bank(PACK * u + t, HALF) for t in range(PACK)] for u in range(2)]
         for g, u in ((1, 0), (1, 1), (2, 0), (0, 0), (2, 1), (0, 1)):
@@ -243,11 +262,11 @@ def tile_list_rvq_gelu_mix_gelu_kernel(
         v_w[0, 1] = gather_words(0, 1)
         v_s[0, 1] = gather_scales(0, 1)
 
-        act0 = activate(acc[0], placed([P, PACK, HALF], F32, "act00", 13 * HALF))
-        act1 = activate(acc[1], kept([P, PACK, HALF], F32, "act10"))
+        act0 = activate(acc[0], placed([P, PACK, HALF], F32, "act00", 13 * HALF), PACK)
+        act1 = activate(acc[1], kept([P, PACK, HALF], F32, "act10"), 2)
         grouped = keep.tile([P, 2 * HALF * PACK], BF16, name="h0", tag="tab_s", align_bytes=64)
-        smooth_on_vector(grouped[:, : HALF * PACK], act0[:], 0)
-        interleave(grouped[:, HALF * PACK :], smooth_rows(act1[:], 1, "smoothed0")[:])
+        interleave(grouped[:, : HALF * PACK], smooth_rows_on_gpsimd(act0[:], 0, "smoothed00")[:])
+        interleave(grouped[:, HALF * PACK :], smooth_rows(act1[:], 1, "smoothed10")[:])
         codes = kept([P, 2 * HALF], U32, "h_codes0")
         plane = kept([P, 2 * HALF], U8, "h_scales0")
         nc.vector.quantize_mx(codes[:].bitcast(FP8X4), plane[:], grouped[:])
@@ -258,13 +277,13 @@ def tile_list_rvq_gelu_mix_gelu_kernel(
             first_layer_pass(acc[u], g, u, 1)
         act0 = activate(acc[0], kept([P, PACK, HALF], F32, "act01"))
         act1 = activate(acc[1], kept([P, PACK, HALF], F32, "act11"))
-        rows = smooth_rows(act1[:, :, :QUARTER], 1, "smoothed1")
+        rows = smooth_rows(act1[:, :, QUARTER:], 1, "smoothed1")
 
         def fill_last(grouped, cols):
             if cols.start == 0:
-                interleave(grouped, rows[:])
-            else:
                 smooth_on_vector(grouped, act1[:, :, cols], 1)
+            else:
+                interleave(grouped, rows[:, :, cols.start - QUARTER : cols.stop - QUARTER])
 
         h8 = quantise_in_pieces(lambda grouped, cols: smooth_on_vector(grouped, act0[:, :, cols], 0), [QUARTER, QUARTER], "01")
         h4 = quantise_in_pieces(fill_last, [QUARTER, P, P], "11")

@@ -195,16 +195,14 @@ def tile_list_rvq_gelu_mix_gelu_kernel(
                 MULT,
             )
 
-        def smooth_rows(act, u, name):
+        def smooth_rows(act, u, rows_on_gpsimd, name):
             rows = kept([P, PACK, act.shape[2]], BF16, name)
             for t in range(PACK):
-                nc.scalar.activation(rows[:, t, :], act[:, t, :], COPY, scale=sm_sb[:, u, t : t + 1])
-            return rows
-
-        def smooth_rows_on_gpsimd(act, u, name):
-            rows = kept([P, PACK, act.shape[2]], BF16, name)
-            for t in range(PACK):
-                nc.gpsimd.tensor_scalar(rows[:, t, :], act[:, t, :], sm_sb[:, u, t : t + 1], 0.0, MULT, ADD)
+                factor = sm_sb[:, u, t : t + 1]
+                if t < rows_on_gpsimd:
+                    nc.gpsimd.tensor_scalar(rows[:, t, :], act[:, t, :], factor, 0.0, MULT, ADD)
+                else:
+                    nc.scalar.activation(rows[:, t, :], act[:, t, :], COPY, scale=factor)
             return rows
 
         def interleave(grouped, rows):
@@ -263,10 +261,10 @@ def tile_list_rvq_gelu_mix_gelu_kernel(
         v_s[0, 1] = gather_scales(0, 1)
 
         act0 = activate(acc[0], placed([P, PACK, HALF], F32, "act00", 13 * HALF), PACK)
-        act1 = activate(acc[1], kept([P, PACK, HALF], F32, "act10"), 2)
+        act1 = activate(acc[1], kept([P, PACK, HALF], F32, "act10"), 1)
         grouped = keep.tile([P, 2 * HALF * PACK], BF16, name="h0", tag="tab_s", align_bytes=64)
-        interleave(grouped[:, : HALF * PACK], smooth_rows_on_gpsimd(act0[:], 0, "smoothed00")[:])
-        interleave(grouped[:, HALF * PACK :], smooth_rows(act1[:], 1, "smoothed10")[:])
+        interleave(grouped[:, : HALF * PACK], smooth_rows(act0[:], 0, PACK, "smoothed00")[:])
+        interleave(grouped[:, HALF * PACK :], smooth_rows(act1[:], 1, 2, "smoothed10")[:])
         codes = kept([P, 2 * HALF], U32, "h_codes0")
         plane = kept([P, 2 * HALF], U8, "h_scales0")
         nc.vector.quantize_mx(codes[:].bitcast(FP8X4), plane[:], grouped[:])
@@ -277,7 +275,7 @@ def tile_list_rvq_gelu_mix_gelu_kernel(
             first_layer_pass(acc[u], g, u, 1)
         act0 = activate(acc[0], kept([P, PACK, HALF], F32, "act01"))
         act1 = activate(acc[1], kept([P, PACK, HALF], F32, "act11"))
-        rows = smooth_rows(act1[:, :, QUARTER:], 1, "smoothed1")
+        rows = smooth_rows(act1[:, :, QUARTER:], 1, 0, "smoothed1")
 
         def fill_last(grouped, cols):
             if cols.start == 0:

@@ -22,6 +22,7 @@ P = 128
 PACK = 4
 HALF = 512
 QUARTER = 256
+KB = 1024
 
 
 def tile_list_rvq_gelu_mix_gelu_kernel(
@@ -40,119 +41,92 @@ def tile_list_rvq_gelu_mix_gelu_kernel(
         def placed(shape, dtype, name, offset):
             return reused.tile(shape, dtype, name=name, offset=offset, align_bytes=64)
 
-        offsets = keep.tile([P, 3 * J // 16], U16, name="offsets")
-        nc.sync.dma_start(offsets[:], offs)
-
         def load_scale_rows(scales, plane):
             for q in range(4):
                 nc.sync.dma_start(
                     plane[32 * q : 32 * q + 4, :].bitcast(I32), scales[0, 4 * q : 4 * q + 4, :].bitcast(I32)
                 )
 
+        W0_LOW, ACT0, W0_HIGH = 0, 8 * KB, 15 * KB
+        W1S_RAW, W2S_RAW, ROWS = 26 * KB, 27 * KB, 28 * KB
+
+        offsets = keep.tile([P, 3 * J // 16], U16, name="offsets")
+        nc.sync.dma_start(offsets[:], offs)
         tab_s = kept([P, T], U8, "tab_s")
         nc.vector.memset(tab_s[:].bitcast(I32), 0)
         load_scale_rows(tab_scales, tab_s[:])
-
-        w_raw = [kept([P, 2 * R], U8, f"w{g}_raw") for g in (1, 2)]
-        ws_raw = [placed([P, R], U8, "w1_s_raw", 3 * HALF), kept([P, R], U8, "w2_s_raw")]
-        wd8_s = kept([P, N], U8, "wd8_s")
-        wd4_s = kept([P, N], U8, "wd4_s")
-        for plane in ws_raw + [wd8_s, wd4_s]:
-            nc.vector.memset(plane[:].bitcast(I32), 0)
-
-        for raw, words in zip(w_raw, (w1_words, w2_words)):
-            nc.sync.dma_start(raw[:].bitcast(I32), words[0].bitcast(I32))
-        tab_w = kept([P, T], I32, "tab_w")
-        nc.sync.dma_start(tab_w[:], tab_words[0].rearrange("p t i -> p (t i)").bitcast(I32))
-        load_scale_rows(w1_scales, ws_raw[0][:])
-
-        w0_rows = w0.rearrange("(p i) r -> p i r", i=PACK)
-        w0_raw = [
-            kept([P, PACK, QUARTER], F32, "w0_raw0"),
-            placed([P, PACK, QUARTER], F32, "w0_raw1", 32 * HALF),
-            kept([P, PACK, QUARTER], F32, "w0_raw2"),
-            placed([P, PACK, QUARTER], F32, "w0_raw3", 8 * HALF),
-        ]
-        for c in range(4):
-            nc.sync.dma_start(w0_raw[c][:], w0_rows[:, :, c * QUARTER : (c + 1) * QUARTER])
-            if c == 1:
-                load_scale_rows(w2_scales, ws_raw[1][:])
-        sm_sb = kept([P, 2, PACK], F32, "sm_sb")
-        nc.sync.dma_start(sm_sb[:], sm.rearrange("(u p t) -> p u t", u=2, t=PACK))
-
-        wd8_w = kept([P, N], I32, "wd8_w")
-        nc.sync.dma_start(wd8_w[:], wd8_words[0].rearrange("p n i -> p (n i)").bitcast(I32))
+        w1_raw = kept([P, 2 * R], U8, "w1_raw")
+        nc.sync.dma_start(w1_raw[:].bitcast(I32), w1_words[0].bitcast(I32))
         wd4_w = kept([P, 2 * N], U8, "wd4_w")
         nc.sync.dma_start(wd4_w[:].bitcast(I32), wd4_words[0].bitcast(I32))
-        load_scale_rows(wd8_scales, wd8_s[:])
-        load_scale_rows(wd4_scales, wd4_s[:])
-        b_sb = kept([P, 2], F32, "b_sb")
-        with nc.allow_non_contiguous_dma(reason="one bias value to a partition"):
-            nc.sync.dma_start(b_sb[:], b.rearrange("(n p) -> p n", p=P))
+        tab_w = kept([P, T], I32, "tab_w")
+        nc.sync.dma_start(tab_w[:], tab_words[0].rearrange("p t i -> p (t i)").bitcast(I32))
+
+        w1s_raw = placed([P, R], U8, "w1s_raw", W1S_RAW)
+        nc.vector.memset(w1s_raw[:].bitcast(I32), 0)
+        load_scale_rows(w1_scales, w1s_raw[:])
+        w2s_raw = placed([P, R], U8, "w2s_raw", W2S_RAW)
+        nc.vector.memset(w2s_raw[:].bitcast(I32), 0)
+        wd_s = kept([P, 2 * N], U8, "wd_s")
+        nc.vector.memset(wd_s[:].bitcast(I32), 0)
 
         zero = kept([P, 1], F32, "zero")
         nc.vector.memset(zero[:], 0.0)
-        no_bias = keep.tile([P, 1], F32, name="no_bias", tag="no_bias", align_bytes=64)
+        no_bias = kept([P, 1], F32, "no_bias")
         nc.scalar.activation(no_bias[:], zero[:], GELU)
 
         def offsets_of(g, half):
             first = (g * J + half * HALF) // 16
             return offsets[:, first : first + HALF // 16]
 
-        def gather_scales(g, half):
-            if (g, half) == (2, 1):
-                picked = placed([P, HALF], U8, "picked_s2_1", 8 * HALF)
-            else:
-                tag = "no_bias" if (g, half) == (0, 1) else f"picked_s{g}_{half}"
-                picked = keep.tile([P, HALF], U8, name="picked_s", tag=tag, align_bytes=64)
+        v_s, v_w, w_codes, w_scales = {}, {}, {}, {}
+
+        def gather_scales(g, half, offset=None):
+            name = f"picked_s{g}_{half}"
+            picked = kept([P, HALF], U8, name) if offset is None else placed([P, HALF], U8, name, offset)
             nc.vector.tensor_copy(picked[:], tab_s[:].indirect(offsets_of(g, half)))
-            return picked
+            v_s[g, half] = picked
 
-        word_places = {(2, 0): 0, (0, 0): 4 * HALF, (1, 1): 33 * HALF, (0, 1): 9 * HALF}
-        word_tags = {(1, 0): "picked_w1_0", (2, 1): "w0_raw2"}
+        def gather_words(g, half, picked):
+            nc.vector.tensor_copy(picked, tab_w[:].bitcast(U32).indirect(offsets_of(g, half)))
+            v_w[g, half] = picked
 
-        def gather_words(g, half):
-            if (g, half) in word_places:
-                picked = placed([P, HALF], U32, f"picked_w{g}_{half}", word_places[g, half])
-            else:
-                picked = keep.tile([P, HALF], U32, name="picked_w", tag=word_tags[g, half], align_bytes=64)
-            nc.vector.tensor_copy(picked[:], tab_w[:].bitcast(U32).indirect(offsets_of(g, half)))
-            return picked
-
-        order = (1, 2, 0)
-        v_s = {(g, 0): gather_scales(g, 0) for g in order}
-
-        v_s[1, 1] = gather_scales(1, 1)
-        w_codes, w_scales, v_w = {}, {}, {}
-        for g, raw in zip((1, 2), w_raw):
-            codes = kept([P, 2 * R], U8, f"w{g}_codes")
-            nc.vector.tensor_copy(
-                codes[:].bitcast(U16).rearrange("p (u t m) -> p u t m", u=2, t=PACK),
-                raw[:].bitcast(U16).rearrange("p (u m t) -> p u t m", u=2, t=PACK),
+        def deal_words(g, u, raw, codes):
+            nc.gpsimd.tensor_copy(
+                codes[:].rearrange("p (t m e) -> p t m e", t=PACK, e=2),
+                raw[:, 2 * u * HALF : 2 * (u + 1) * HALF].rearrange("p (m t e) -> p t m e", t=PACK, e=2),
             )
-            for u in range(2):
-                for t in range(PACK):
-                    first = u * HALF + t * P
-                    w_codes[g, u, t] = codes[:, 2 * first : 2 * (first + P)].bitcast(FP4X4)
+            for t in range(PACK):
+                w_codes[g, u, t] = codes[:, 2 * t * P : 2 * (t + 1) * P].bitcast(FP4X4)
 
-        def deal_scales(g, units, plane):
-            raw_s = ws_raw[g - 1][:, units[0] * HALF : (units[-1] + 1) * HALF]
-            nc.vector.tensor_copy(
-                plane[:].rearrange("p (u t m) -> p u t m", t=PACK, m=P),
-                raw_s.rearrange("p (u m t) -> p u t m", t=PACK, m=P),
+        def deal_scales(g, u, raw):
+            plane = kept([P, HALF], U8, f"w{g}_scales{u}")
+            nc.gpsimd.tensor_copy(
+                plane[:].rearrange("p (t m) -> p t m", t=PACK),
+                raw[:, u * HALF : (u + 1) * HALF].rearrange("p (m t) -> p t m", t=PACK),
             )
-            for i, u in enumerate(units):
-                for t in range(PACK):
-                    first = i * HALF + t * P
-                    w_scales[g, u, t] = plane[:, first : first + P]
+            for t in range(PACK):
+                w_scales[g, u, t] = plane[:, t * P : (t + 1) * P]
 
-        def quantise_w0(u):
+        w0_rows = w0.rearrange("(p i) r -> p i r", i=PACK)
+
+        def load_w0(u, offset):
+            raw = placed([P, 2, PACK, QUARTER], F32, f"w0_raw{u}", offset)
+            for c in range(2):
+                first = u * HALF + c * QUARTER
+                nc.sync.dma_start(raw[:, c], w0_rows[:, :, first : first + QUARTER])
+            return raw
+
+        def round_w0(u, raw):
             grouped = kept([P, HALF * PACK], BF16, f"w0_grouped{u}")
             dealt = grouped[:].rearrange("p (a e m i) -> p a m i e", a=2, e=2, i=PACK)
             for c in range(2):
-                src = w0_raw[2 * u + c][:].rearrange("p i (m a e) -> p a m i e", a=2, e=2)
+                src = raw[:, c].rearrange("p i (m a e) -> p a m i e", a=2, e=2)
                 for a in range(2):
                     nc.scalar.copy(dealt[:, a, c * 64 : (c + 1) * 64], src[:, a])
+            return grouped
+
+        def quantise_w0(u, grouped):
             codes = kept([P, HALF], U32, f"w0_codes{u}")
             plane = kept([P, HALF], U8, f"w0_scales{u}")
             nc.vector.quantize_mx(codes[:].bitcast(FP8X4), plane[:], grouped[:])
@@ -160,25 +134,54 @@ def tile_list_rvq_gelu_mix_gelu_kernel(
                 w_codes[0, u, t] = codes[:, t * P : (t + 1) * P].bitcast(FP8X4)
                 w_scales[0, u, t] = plane[:, t * P : (t + 1) * P]
 
-        deal_scales(1, (0, 1), kept([P, R], U8, "w1_scales"))
-        deal_scales(2, (0,), kept([P, HALF], U8, "w2_scales0"))
-        for g in order:
-            v_w[g, 0] = gather_words(g, 0)
-        quantise_w0(0)
-        deal_scales(2, (1,), placed([P, HALF], U8, "w2_scales1", 32 * HALF))
-        quantise_w0(1)
+        w2_raw = kept([P, 2 * R], U8, "w2_raw")
+        nc.sync.dma_start(w2_raw[:].bitcast(I32), w2_words[0].bitcast(I32))
+        w0_low = load_w0(0, W0_LOW)
+        load_scale_rows(w2_scales, w2s_raw[:])
+        w0_high = load_w0(1, W0_HIGH)
+        wd8_w = kept([P, N], I32, "wd8_w")
+        nc.sync.dma_start(wd8_w[:], wd8_words[0].rearrange("p n i -> p (n i)").bitcast(I32))
+        sm_sb = kept([P, 2, PACK], F32, "sm_sb")
+        nc.sync.dma_start(sm_sb[:], sm.rearrange("(u p t) -> p u t", u=2, t=PACK))
+        wd8_s, wd4_s = wd_s[:, :N], wd_s[:, N:]
+        load_scale_rows(wd8_scales, wd8_s)
+        load_scale_rows(wd4_scales, wd4_s)
+        b_sb = kept([P, 2], F32, "b_sb")
+        with nc.allow_non_contiguous_dma(reason="one bias value to a partition"):
+            nc.sync.dma_start(b_sb[:], b.rearrange("(n p) -> p n", p=P))
+
+        for u in range(2):
+            deal_words(1, u, w1_raw, kept([P, 2 * HALF], U8, f"w1_codes{u}"))
+        for u in range(2):
+            deal_scales(1, u, w1s_raw)
+        deal_words(2, 0, w2_raw, placed([P, 2 * HALF], U8, "w2_codes0", W1S_RAW))
+        for u in range(2):
+            deal_scales(2, u, w2s_raw)
+        deal_words(2, 1, w2_raw, placed([P, 2 * HALF], U8, "w2_codes1", W2S_RAW))
+        for g, half in ((1, 0), (2, 0), (0, 0), (1, 1)):
+            gather_scales(g, half)
+        for g, half in ((1, 0), (2, 0), (0, 0), (1, 1)):
+            gather_words(g, half, kept([P, HALF], U32, f"picked_w{g}_{half}")[:])
+
+        grouped_low = round_w0(0, w0_low)
+        grouped_high = round_w0(1, w0_high)
+        quantise_w0(0, grouped_low)
+        gather_scales(2, 1, W0_LOW)
+        quantise_w0(1, grouped_high)
+        gather_words(2, 1, placed([P, HALF], U32, "picked_w2_1", W0_HIGH + 2 * KB)[:])
+        gather_scales(0, 1, W0_HIGH + KB)
+        gather_words(0, 1, placed([P, HALF], U32, "picked_w0_1", W0_HIGH + 4 * KB)[:])
 
         def bank(index, width):
             tile = psum.tile([P, HALF], F32, name="bank", tag=f"bank{index}")
             return tile[:, :width]
 
-        def first_layer_pass(acc, g, u, half):
-            for t in range(PACK):
-                nc.tensor.matmul_mx(
-                    acc[t], lhsT=w_codes[g, u, t], lhsT_scale=w_scales[g, u, t],
-                    rhs=v_w[g, half][:].bitcast(FP8X4), rhs_scale=v_s[g, half][:],
-                    start=(g == order[0]), stop=(g == order[-1]),
-                )
+        def first_layer_pass(acc, g, u, t, half):
+            nc.tensor.matmul_mx(
+                acc[u][t], lhsT=w_codes[g, u, t], lhsT_scale=w_scales[g, u, t],
+                rhs=v_w[g, half].bitcast(FP8X4), rhs_scale=v_s[g, half][:],
+                start=(g == 1), stop=(g == 0),
+            )
 
         def activate(acc, act, with_bias_tile=0):
             for t in range(PACK):
@@ -195,8 +198,7 @@ def tile_list_rvq_gelu_mix_gelu_kernel(
                 MULT,
             )
 
-        def smooth_rows(act, u, rows_on_gpsimd, name):
-            rows = kept([P, PACK, act.shape[2]], BF16, name)
+        def smooth_rows(act, u, rows_on_gpsimd, rows):
             for t in range(PACK):
                 factor = sm_sb[:, u, t : t + 1]
                 if t < rows_on_gpsimd:
@@ -211,21 +213,11 @@ def tile_list_rvq_gelu_mix_gelu_kernel(
                 rows.rearrange("p t (c e) -> p c t e", e=PACK),
             )
 
-        def quantise_in_pieces(fill, widths, name):
-            codes = kept([P, HALF], U32, f"h_codes{name}")
-            plane = kept([P, HALF], U8, f"h_scales{name}")
-            pieces = [slice(sum(widths[:c]), sum(widths[: c + 1])) for c in range(len(widths))]
-            grouped = [kept([P, w * PACK], BF16, f"h{name}{c}") for c, w in enumerate(widths)]
+        def h_tiles(name):
+            return kept([P, HALF], U32, f"h_codes{name}"), kept([P, HALF], U8, f"h_scales{name}")
 
-            def quantise(c):
-                nc.vector.quantize_mx(codes[:, pieces[c]].bitcast(FP8X4), plane[:, pieces[c]], grouped[c][:])
-
-            for c, cols in enumerate(pieces):
-                fill(grouped[c][:], cols)
-                if c > 0:
-                    quantise(c - 1)
-            quantise(len(pieces) - 1)
-            return codes[:], plane[:], pieces
+        def quantise_h(h, cols, grouped):
+            nc.vector.quantize_mx(h[0][:, cols].bitcast(FP8X4), h[1][:, cols], grouped)
 
         def second_layer(banks, h8, h4, cols, j_first, name):
             width = cols.stop - cols.start
@@ -252,39 +244,45 @@ def tile_list_rvq_gelu_mix_gelu_kernel(
 
         acc = [[bank(PACK * u + t, HALF) for t in range(PACK)] for u in range(2)]
         for g, u in ((1, 0), (1, 1), (2, 0), (0, 0), (2, 1), (0, 1)):
-            first_layer_pass(acc[u], g, u, 0)
-
-        v_w[1, 1] = gather_words(1, 1)
-        v_w[2, 1] = gather_words(2, 1)
-        v_s[2, 1] = gather_scales(2, 1)
-        v_w[0, 1] = gather_words(0, 1)
-        v_s[0, 1] = gather_scales(0, 1)
-
-        act0 = activate(acc[0], placed([P, PACK, HALF], F32, "act00", 13 * HALF), PACK)
-        act1 = activate(acc[1], kept([P, PACK, HALF], F32, "act10"), 1)
-        grouped = keep.tile([P, 2 * HALF * PACK], BF16, name="h0", tag="tab_s", align_bytes=64)
-        interleave(grouped[:, : HALF * PACK], smooth_rows(act0[:], 0, PACK, "smoothed00")[:])
-        interleave(grouped[:, HALF * PACK :], smooth_rows(act1[:], 1, 2, "smoothed10")[:])
-        codes = kept([P, 2 * HALF], U32, "h_codes0")
-        plane = kept([P, 2 * HALF], U8, "h_scales0")
-        nc.vector.quantize_mx(codes[:].bitcast(FP8X4), plane[:], grouped[:])
-        h_first = [(codes[:, u * HALF : (u + 1) * HALF], plane[:, u * HALF : (u + 1) * HALF]) for u in range(2)]
+            for t in range(PACK):
+                first_layer_pass(acc, g, u, t, 0)
+        act0 = activate(acc[0], placed([P, PACK, HALF], F32, "act00", ACT0), 1)
+        act1 = activate(acc[1], kept([P, PACK, HALF], F32, "act10"))
+        rows = [smooth_rows(act0[:], 0, PACK, kept([P, PACK, HALF], BF16, "smoothed00")),
+                smooth_rows(act1[:], 1, 2, placed([P, PACK, HALF], BF16, "smoothed10", ROWS))]
+        grouped = [kept([P, HALF * PACK], BF16, f"h0{u}") for u in range(2)]
+        h_first = [h_tiles(f"0{u}") for u in range(2)]
+        for u in range(2):
+            interleave(grouped[u][:], rows[u][:])
+        for u in range(2):
+            quantise_h(h_first[u], slice(0, HALF), grouped[u][:])
 
         acc = [[bank(PACK * u + t, HALF) for t in range(PACK)] for u in range(2)]
-        for g, u in ((1, 0), (2, 0), (1, 1), (0, 0), (2, 1), (0, 1)):
-            first_layer_pass(acc[u], g, u, 1)
+        for g in (1, 2, 0):
+            for t in range(PACK):
+                first_layer_pass(acc, g, 0, t, 1)
+        for t in range(PACK):
+            for g in (1, 2, 0):
+                first_layer_pass(acc, g, 1, t, 1)
         act0 = activate(acc[0], kept([P, PACK, HALF], F32, "act01"))
         act1 = activate(acc[1], kept([P, PACK, HALF], F32, "act11"))
-        rows = smooth_rows(act1[:, :, QUARTER:], 1, 0, "smoothed1")
+        rows = smooth_rows(act1[:, :, QUARTER:], 1, 0, kept([P, PACK, QUARTER], BF16, "smoothed1"))
 
-        def fill_last(grouped, cols):
-            if cols.start == 0:
-                smooth_on_vector(grouped, act1[:, :, cols], 1)
+        h8, h4 = h_tiles("10"), h_tiles("11")
+        pieces = [(0, slice(0, QUARTER)), (0, slice(QUARTER, HALF)), (1, slice(0, QUARTER)),
+                  (1, slice(QUARTER, QUARTER + P)), (1, slice(QUARTER + P, HALF))]
+        h_second = placed([P, 2, HALF * PACK], BF16, "h1", ROWS)
+        waiting = None
+        for u, cols in pieces:
+            grouped = h_second[:, u, cols.start * PACK : cols.stop * PACK]
+            if u == 0 or cols.start == 0:
+                smooth_on_vector(grouped, (act0, act1)[u][:, :, cols], u)
             else:
                 interleave(grouped, rows[:, :, cols.start - QUARTER : cols.stop - QUARTER])
-
-        h8 = quantise_in_pieces(lambda grouped, cols: smooth_on_vector(grouped, act0[:, :, cols], 0), [QUARTER, QUARTER], "01")
-        h4 = quantise_in_pieces(fill_last, [QUARTER, P, P], "11")
+            if waiting:
+                quantise_h(*waiting)
+            waiting = ((h8, h4)[u], cols, grouped)
+        quantise_h(*waiting)
         second_layer((0, 1), h_first[0], h_first[1], slice(0, HALF), 0, "0")
-        for c, cols in enumerate(h4[2]):
+        for c, (u, cols) in enumerate(pieces[2:]):
             second_layer((2 + 2 * c, 3 + 2 * c), h8, h4, cols, HALF, f"1{c}")

@@ -1,6 +1,7 @@
 from contextlib import ExitStack
 
 import concourse.mybir as mybir
+from concourse.masks import make_identity
 
 K, R, N, T, J = 512, 1024, 256, 4096, 1024
 FLOPS = 2 * (3 * K * R * J + R * N * J)
@@ -23,6 +24,7 @@ PACK = 4
 HALF = 512
 QUARTER = 256
 KB = 1024
+SCALAR_SHARE = 320
 
 
 def tile_list_rvq_gelu_mix_gelu_kernel(
@@ -48,7 +50,7 @@ def tile_list_rvq_gelu_mix_gelu_kernel(
                 )
 
         W0_LOW, ACT0, W0_HIGH = 0, 8 * KB, 15 * KB
-        W1S_RAW, W2S_RAW, ROWS = 26 * KB, 27 * KB, 28 * KB
+        GROUPED, W2S_RAW, ROWS, NO_BIAS = 23 * KB, 27 * KB, 32 * KB, 40 * KB
 
         offsets = keep.tile([P, 3 * J // 16], U16, name="offsets")
         nc.sync.dma_start(offsets[:], offs)
@@ -57,12 +59,12 @@ def tile_list_rvq_gelu_mix_gelu_kernel(
         load_scale_rows(tab_scales, tab_s[:])
         w1_raw = kept([P, 2 * R], U8, "w1_raw")
         nc.sync.dma_start(w1_raw[:].bitcast(I32), w1_words[0].bitcast(I32))
-        wd4_w = kept([P, 2 * N], U8, "wd4_w")
-        nc.sync.dma_start(wd4_w[:].bitcast(I32), wd4_words[0].bitcast(I32))
+        w2_raw = kept([P, 2 * R], U8, "w2_raw")
+        nc.sync.dma_start(w2_raw[:].bitcast(I32), w2_words[0].bitcast(I32))
         tab_w = kept([P, T], I32, "tab_w")
         nc.sync.dma_start(tab_w[:], tab_words[0].rearrange("p t i -> p (t i)").bitcast(I32))
 
-        w1s_raw = placed([P, R], U8, "w1s_raw", W1S_RAW)
+        w1s_raw = kept([P, R], U8, "w1s_raw")
         nc.vector.memset(w1s_raw[:].bitcast(I32), 0)
         load_scale_rows(w1_scales, w1s_raw[:])
         w2s_raw = placed([P, R], U8, "w2s_raw", W2S_RAW)
@@ -72,7 +74,7 @@ def tile_list_rvq_gelu_mix_gelu_kernel(
 
         zero = kept([P, 1], F32, "zero")
         nc.vector.memset(zero[:], 0.0)
-        no_bias = kept([P, 1], F32, "no_bias")
+        no_bias = placed([P, 1], F32, "no_bias", NO_BIAS)
         nc.scalar.activation(no_bias[:], zero[:], GELU)
 
         def offsets_of(g, half):
@@ -85,13 +87,14 @@ def tile_list_rvq_gelu_mix_gelu_kernel(
             name = f"picked_s{g}_{half}"
             picked = kept([P, HALF], U8, name) if offset is None else placed([P, HALF], U8, name, offset)
             nc.vector.tensor_copy(picked[:], tab_s[:].indirect(offsets_of(g, half)))
-            v_s[g, half] = picked
+            v_s[g, half] = picked[:]
 
         def gather_words(g, half, picked):
             nc.vector.tensor_copy(picked, tab_w[:].bitcast(U32).indirect(offsets_of(g, half)))
             v_w[g, half] = picked
 
-        def deal_words(g, u, raw, codes):
+        def deal_words(g, u, raw):
+            codes = kept([P, 2 * HALF], U8, f"w{g}_codes{u}")
             nc.gpsimd.tensor_copy(
                 codes[:].rearrange("p (t m e) -> p t m e", t=PACK, e=2),
                 raw[:, 2 * u * HALF : 2 * (u + 1) * HALF].rearrange("p (m t e) -> p t m e", t=PACK, e=2),
@@ -99,8 +102,7 @@ def tile_list_rvq_gelu_mix_gelu_kernel(
             for t in range(PACK):
                 w_codes[g, u, t] = codes[:, 2 * t * P : 2 * (t + 1) * P].bitcast(FP4X4)
 
-        def deal_scales(g, u, raw):
-            plane = kept([P, HALF], U8, f"w{g}_scales{u}")
+        def deal_scales(g, u, raw, plane):
             nc.gpsimd.tensor_copy(
                 plane[:].rearrange("p (t m) -> p t m", t=PACK),
                 raw[:, u * HALF : (u + 1) * HALF].rearrange("p (m t) -> p t m", t=PACK),
@@ -117,13 +119,18 @@ def tile_list_rvq_gelu_mix_gelu_kernel(
                 nc.sync.dma_start(raw[:, c], w0_rows[:, :, first : first + QUARTER])
             return raw
 
-        def round_w0(u, raw):
-            grouped = kept([P, HALF * PACK], BF16, f"w0_grouped{u}")
+        def round_w0(raw, grouped, on_gpsimd):
             dealt = grouped[:].rearrange("p (a e m i) -> p a m i e", a=2, e=2, i=PACK)
             for c in range(2):
                 src = raw[:, c].rearrange("p i (m a e) -> p a m i e", a=2, e=2)
                 for a in range(2):
-                    nc.scalar.copy(dealt[:, a, c * 64 : (c + 1) * 64], src[:, a])
+                    if (c, a) in on_gpsimd:
+                        nc.gpsimd.tensor_scalar(
+                            dealt[:, a, c * 64 : (c + 1) * 64].rearrange("p m i e -> p e m i"),
+                            src[:, a].rearrange("p m i e -> p e m i"), 1.0, 0.0, MULT, ADD,
+                        )
+                    else:
+                        nc.scalar.copy(dealt[:, a, c * 64 : (c + 1) * 64], src[:, a])
             return grouped
 
         def quantise_w0(u, grouped):
@@ -134,8 +141,6 @@ def tile_list_rvq_gelu_mix_gelu_kernel(
                 w_codes[0, u, t] = codes[:, t * P : (t + 1) * P].bitcast(FP8X4)
                 w_scales[0, u, t] = plane[:, t * P : (t + 1) * P]
 
-        w2_raw = kept([P, 2 * R], U8, "w2_raw")
-        nc.sync.dma_start(w2_raw[:].bitcast(I32), w2_words[0].bitcast(I32))
         w0_low = load_w0(0, W0_LOW)
         load_scale_rows(w2_scales, w2s_raw[:])
         w0_high = load_w0(1, W0_HIGH)
@@ -143,34 +148,45 @@ def tile_list_rvq_gelu_mix_gelu_kernel(
         nc.sync.dma_start(wd8_w[:], wd8_words[0].rearrange("p n i -> p (n i)").bitcast(I32))
         sm_sb = kept([P, 2, PACK], F32, "sm_sb")
         nc.sync.dma_start(sm_sb[:], sm.rearrange("(u p t) -> p u t", u=2, t=PACK))
+        wd4_w = kept([P, 2 * N], U8, "wd4_w")
+        nc.sync.dma_start(wd4_w[:].bitcast(I32), wd4_words[0].bitcast(I32))
         wd8_s, wd4_s = wd_s[:, :N], wd_s[:, N:]
         load_scale_rows(wd8_scales, wd8_s)
         load_scale_rows(wd4_scales, wd4_s)
+        identity = kept([P, P], F32, "identity")
+        make_identity(nc, identity[:])
+        sm_rows = kept([P, P], F32, "sm_rows")
+        nc.gpsimd.memset(sm_rows[:], 0.0)
+        with nc.allow_non_contiguous_dma(reason="row 4 u + t takes every fourth factor"):
+            for u in range(2):
+                nc.sync.dma_start(
+                    sm_rows[PACK * u : PACK * (u + 1), :], sm[u * HALF : (u + 1) * HALF].rearrange("(p t) -> t p", t=PACK)
+                )
         b_sb = kept([P, 2], F32, "b_sb")
         with nc.allow_non_contiguous_dma(reason="one bias value to a partition"):
             nc.sync.dma_start(b_sb[:], b.rearrange("(n p) -> p n", p=P))
 
-        for u in range(2):
-            deal_words(1, u, w1_raw, kept([P, 2 * HALF], U8, f"w1_codes{u}"))
-        for u in range(2):
-            deal_scales(1, u, w1s_raw)
-        deal_words(2, 0, w2_raw, placed([P, 2 * HALF], U8, "w2_codes0", W1S_RAW))
-        for u in range(2):
-            deal_scales(2, u, w2s_raw)
-        deal_words(2, 1, w2_raw, placed([P, 2 * HALF], U8, "w2_codes1", W2S_RAW))
-        for g, half in ((1, 0), (2, 0), (0, 0), (1, 1)):
-            gather_scales(g, half)
-        for g, half in ((1, 0), (2, 0), (0, 0), (1, 1)):
-            gather_words(g, half, kept([P, HALF], U32, f"picked_w{g}_{half}")[:])
+        for g, raw in ((1, w1_raw), (2, w2_raw)):
+            for u in range(2):
+                deal_words(g, u, raw)
+        for g, u, raw in ((1, 0, w1s_raw), (2, 0, w2s_raw), (2, 1, w2s_raw)):
+            deal_scales(g, u, raw, kept([P, HALF], U8, f"w{g}_scales{u}"))
+        early = kept([P, 3 * HALF], U8, "picked_s_early")
+        nc.vector.tensor_copy(early[:], tab_s[:].indirect(offsets[:, J // 16 : (J + 3 * HALF) // 16]))
+        for c, place in enumerate(((1, 0), (1, 1), (2, 0))):
+            v_s[place] = early[:, c * HALF : (c + 1) * HALF]
+        gather_scales(0, 0)
+        for g in (1, 2, 0):
+            gather_words(g, 0, kept([P, HALF], U32, f"picked_w{g}_0")[:])
 
-        grouped_low = round_w0(0, w0_low)
-        grouped_high = round_w0(1, w0_high)
+        grouped_low = round_w0(w0_low, placed([P, HALF * PACK], BF16, "w0_grouped0", GROUPED), ())
+        grouped_high = round_w0(w0_high, placed([P, HALF * PACK], BF16, "w0_grouped1", W2S_RAW + 512), ((1, 0),))
         quantise_w0(0, grouped_low)
-        gather_scales(2, 1, W0_LOW)
+        deal_scales(1, 1, w1s_raw, placed([P, HALF], U8, "w1_scales1", W2S_RAW - 256))
+        gather_words(1, 1, placed([P, HALF], U32, "picked_w1_1", W0_LOW)[:])
         quantise_w0(1, grouped_high)
-        gather_words(2, 1, placed([P, HALF], U32, "picked_w2_1", W0_HIGH + 2 * KB)[:])
+        gather_scales(2, 1, W0_HIGH + KB + HALF)
         gather_scales(0, 1, W0_HIGH + KB)
-        gather_words(0, 1, placed([P, HALF], U32, "picked_w0_1", W0_HIGH + 4 * KB)[:])
 
         def bank(index, width):
             tile = psum.tile([P, HALF], F32, name="bank", tag=f"bank{index}")
@@ -179,18 +195,26 @@ def tile_list_rvq_gelu_mix_gelu_kernel(
         def first_layer_pass(acc, g, u, t, half):
             nc.tensor.matmul_mx(
                 acc[u][t], lhsT=w_codes[g, u, t], lhsT_scale=w_scales[g, u, t],
-                rhs=v_w[g, half].bitcast(FP8X4), rhs_scale=v_s[g, half][:],
+                rhs=v_w[g, half].bitcast(FP8X4), rhs_scale=v_s[g, half],
                 start=(g == 1), stop=(g == 0),
             )
+
+        def first_layer(acc, half):
+            for g in (1, 2, 0):
+                for t in range(PACK):
+                    first_layer_pass(acc, g, 0, t, half)
+            for t in range(PACK):
+                for g in (1, 2, 0):
+                    first_layer_pass(acc, g, 1, t, half)
 
         def activate(acc, act, with_bias_tile=0):
             for t in range(PACK):
                 nc.scalar.activation(act[:, t, :], acc[t], GELU, bias=no_bias[:] if t < with_bias_tile else 0.0)
             return act
 
-        def smooth_on_vector(grouped, act, u):
+        def smooth_on_vector(grouped, act, factors):
             width = act.shape[2]
-            factor = sm_sb[:, u, :].unsqueeze(1).unsqueeze(3).to_broadcast([P, width // 2, PACK, 2])
+            factor = factors.unsqueeze(1).unsqueeze(3).to_broadcast([P, width // 2, PACK, 2])
             nc.vector.tensor_tensor(
                 grouped.rearrange("p (c e t) -> p c t e", e=2, t=PACK),
                 act.rearrange("p t (c e) -> p c t e", e=2),
@@ -207,8 +231,8 @@ def tile_list_rvq_gelu_mix_gelu_kernel(
                     nc.scalar.activation(rows[:, t, :], act[:, t, :], COPY, scale=factor)
             return rows
 
-        def interleave(grouped, rows):
-            nc.vector.tensor_copy(
+        def interleave(grouped, rows, copy=nc.vector.tensor_copy):
+            copy(
                 grouped.rearrange("p (c e t) -> p c t e", e=PACK, t=PACK),
                 rows.rearrange("p t (c e) -> p c t e", e=PACK),
             )
@@ -243,46 +267,48 @@ def tile_list_rvq_gelu_mix_gelu_kernel(
                 nc.sync.dma_start(out[n * P : (n + 1) * P, j_first + cols.start : j_first + cols.stop], result[:])
 
         acc = [[bank(PACK * u + t, HALF) for t in range(PACK)] for u in range(2)]
-        for g, u in ((1, 0), (1, 1), (2, 0), (0, 0), (2, 1), (0, 1)):
-            for t in range(PACK):
-                first_layer_pass(acc, g, u, t, 0)
-        act0 = activate(acc[0], placed([P, PACK, HALF], F32, "act00", ACT0), 1)
+        first_layer(acc, 0)
+        act0 = activate(acc[0], placed([P, PACK, HALF], F32, "act00", ACT0), PACK)
+        late = placed([P, 2, HALF], U32, "picked_late", NO_BIAS)
+        gather_words(2, 1, late[:, 0])
+        gather_words(0, 1, late[:, 1])
         act1 = activate(acc[1], kept([P, PACK, HALF], F32, "act10"))
-        rows = [smooth_rows(act0[:], 0, PACK, kept([P, PACK, HALF], BF16, "smoothed00")),
-                smooth_rows(act1[:], 1, 2, placed([P, PACK, HALF], BF16, "smoothed10", ROWS))]
+        rows = [smooth_rows(act0[:], 0, PACK, placed([P, PACK, HALF], BF16, "smoothed00", W2S_RAW + 512)),
+                smooth_rows(act1[:], 1, 3, placed([P, PACK, HALF], BF16, "smoothed10", ROWS))]
         grouped = [kept([P, HALF * PACK], BF16, f"h0{u}") for u in range(2)]
         h_first = [h_tiles(f"0{u}") for u in range(2)]
-        for u in range(2):
-            interleave(grouped[u][:], rows[u][:])
+        interleave(grouped[0][:, : SCALAR_SHARE * PACK], rows[0][:, :, :SCALAR_SHARE], nc.scalar.copy)
+        interleave(grouped[0][:, SCALAR_SHARE * PACK :], rows[0][:, :, SCALAR_SHARE:])
+        interleave(grouped[1][:], rows[1][:])
         for u in range(2):
             quantise_h(h_first[u], slice(0, HALF), grouped[u][:])
 
         acc = [[bank(PACK * u + t, HALF) for t in range(PACK)] for u in range(2)]
-        for g in (1, 2, 0):
-            for t in range(PACK):
-                first_layer_pass(acc, g, 0, t, 1)
-        for t in range(PACK):
-            for g in (1, 2, 0):
-                first_layer_pass(acc, g, 1, t, 1)
+        first_layer(acc, 1)
         act0 = activate(acc[0], kept([P, PACK, HALF], F32, "act01"))
+        sm_bank = bank(2, P)
+        nc.tensor.transpose(sm_bank, sm_rows[:], identity[:])
         act1 = activate(acc[1], kept([P, PACK, HALF], F32, "act11"))
-        rows = smooth_rows(act1[:, :, QUARTER:], 1, 0, kept([P, PACK, QUARTER], BF16, "smoothed1"))
-
         h8, h4 = h_tiles("10"), h_tiles("11")
-        pieces = [(0, slice(0, QUARTER)), (0, slice(QUARTER, HALF)), (1, slice(0, QUARTER)),
-                  (1, slice(QUARTER, QUARTER + P)), (1, slice(QUARTER + P, HALF))]
         h_second = placed([P, 2, HALF * PACK], BF16, "h1", ROWS)
-        waiting = None
-        for u, cols in pieces:
-            grouped = h_second[:, u, cols.start * PACK : cols.stop * PACK]
-            if u == 0 or cols.start == 0:
-                smooth_on_vector(grouped, (act0, act1)[u][:, :, cols], u)
-            else:
-                interleave(grouped, rows[:, :, cols.start - QUARTER : cols.stop - QUARTER])
-            if waiting:
-                quantise_h(*waiting)
-            waiting = ((h8, h4)[u], cols, grouped)
-        quantise_h(*waiting)
+
+        def grouped_cols(u, cols):
+            return h_second[:, u, cols.start * PACK : cols.stop * PACK]
+
+        first, rest = slice(0, QUARTER), slice(QUARTER, HALF)
+        third, last = slice(QUARTER, QUARTER + P), slice(QUARTER + P, HALF)
+        smooth_on_vector(grouped_cols(0, first), act0[:, :, first], sm_bank[:, :PACK])
+        rows = smooth_rows(act0[:, :, rest], 0, PACK, kept([P, PACK, QUARTER], BF16, "smoothed01"))
+        interleave(grouped_cols(0, rest), rows[:])
+        quantise_h(h8, first, grouped_cols(0, first))
+        quantise_h(h8, rest, grouped_cols(0, rest))
+        smooth_on_vector(grouped_cols(1, first), act1[:, :, first], sm_bank[:, PACK : 2 * PACK])
+        pieces = [first, third, last]
+        for before, cols, rows_on_gpsimd in ((first, third, PACK), (third, last, 0)):
+            rows = smooth_rows(act1[:, :, cols], 1, rows_on_gpsimd, kept([P, PACK, P], BF16, f"smoothed1{cols.start}"))
+            interleave(grouped_cols(1, cols), rows[:])
+            quantise_h(h4, before, grouped_cols(1, before))
+        quantise_h(h4, last, grouped_cols(1, last))
         second_layer((0, 1), h_first[0], h_first[1], slice(0, HALF), 0, "0")
-        for c, (u, cols) in enumerate(pieces[2:]):
-            second_layer((2 + 2 * c, 3 + 2 * c), h8, h4, cols, HALF, f"1{c}")
+        for c, (cols, banks) in enumerate(zip(pieces, ((3, 4), (5, 6), (7, 0)))):
+            second_layer(banks, h8, h4, cols, HALF, f"1{c}")

@@ -1,7 +1,6 @@
 from contextlib import ExitStack
 
 import concourse.mybir as mybir
-from concourse.masks import make_identity
 
 K, R, N, T, J = 512, 1024, 256, 4096, 1024
 FLOPS = 2 * (3 * K * R * J + R * N * J)
@@ -24,7 +23,8 @@ PACK = 4
 HALF = 512
 QUARTER = 256
 KB = 1024
-SCALAR_SHARE = 320
+GPSIMD_SHARE = 256
+WARM_UPS = 3
 
 
 def tile_list_rvq_gelu_mix_gelu_kernel(
@@ -119,18 +119,12 @@ def tile_list_rvq_gelu_mix_gelu_kernel(
                 nc.sync.dma_start(raw[:, c], w0_rows[:, :, first : first + QUARTER])
             return raw
 
-        def round_w0(raw, grouped, on_gpsimd):
+        def round_w0(raw, grouped):
             dealt = grouped[:].rearrange("p (a e m i) -> p a m i e", a=2, e=2, i=PACK)
             for c in range(2):
                 src = raw[:, c].rearrange("p i (m a e) -> p a m i e", a=2, e=2)
                 for a in range(2):
-                    if (c, a) in on_gpsimd:
-                        nc.gpsimd.tensor_scalar(
-                            dealt[:, a, c * 64 : (c + 1) * 64].rearrange("p m i e -> p e m i"),
-                            src[:, a].rearrange("p m i e -> p e m i"), 1.0, 0.0, MULT, ADD,
-                        )
-                    else:
-                        nc.scalar.copy(dealt[:, a, c * 64 : (c + 1) * 64], src[:, a])
+                    nc.scalar.copy(dealt[:, a, c * 64 : (c + 1) * 64], src[:, a])
             return grouped
 
         def quantise_w0(u, grouped):
@@ -153,15 +147,6 @@ def tile_list_rvq_gelu_mix_gelu_kernel(
         wd8_s, wd4_s = wd_s[:, :N], wd_s[:, N:]
         load_scale_rows(wd8_scales, wd8_s)
         load_scale_rows(wd4_scales, wd4_s)
-        identity = kept([P, P], F32, "identity")
-        make_identity(nc, identity[:])
-        sm_rows = kept([P, P], F32, "sm_rows")
-        nc.gpsimd.memset(sm_rows[:], 0.0)
-        with nc.allow_non_contiguous_dma(reason="row 4 u + t takes every fourth factor"):
-            for u in range(2):
-                nc.sync.dma_start(
-                    sm_rows[PACK * u : PACK * (u + 1), :], sm[u * HALF : (u + 1) * HALF].rearrange("(p t) -> t p", t=PACK)
-                )
         b_sb = kept([P, 2], F32, "b_sb")
         with nc.allow_non_contiguous_dma(reason="one bias value to a partition"):
             nc.sync.dma_start(b_sb[:], b.rearrange("(n p) -> p n", p=P))
@@ -179,8 +164,8 @@ def tile_list_rvq_gelu_mix_gelu_kernel(
         for g in (1, 2, 0):
             gather_words(g, 0, kept([P, HALF], U32, f"picked_w{g}_0")[:])
 
-        grouped_low = round_w0(w0_low, placed([P, HALF * PACK], BF16, "w0_grouped0", GROUPED), ())
-        grouped_high = round_w0(w0_high, placed([P, HALF * PACK], BF16, "w0_grouped1", W2S_RAW + 512), ((1, 0),))
+        grouped_low = round_w0(w0_low, placed([P, HALF * PACK], BF16, "w0_grouped0", GROUPED))
+        grouped_high = round_w0(w0_high, placed([P, HALF * PACK], BF16, "w0_grouped1", W2S_RAW + KB))
         quantise_w0(0, grouped_low)
         deal_scales(1, 1, w1s_raw, placed([P, HALF], U8, "w1_scales1", W2S_RAW - 256))
         gather_words(1, 1, placed([P, HALF], U32, "picked_w1_1", W0_LOW)[:])
@@ -212,9 +197,9 @@ def tile_list_rvq_gelu_mix_gelu_kernel(
                 nc.scalar.activation(act[:, t, :], acc[t], GELU, bias=no_bias[:] if t < with_bias_tile else 0.0)
             return act
 
-        def smooth_on_vector(grouped, act, factors):
+        def smooth_on_vector(grouped, act, u):
             width = act.shape[2]
-            factor = factors.unsqueeze(1).unsqueeze(3).to_broadcast([P, width // 2, PACK, 2])
+            factor = sm_sb[:, u, :].unsqueeze(1).unsqueeze(3).to_broadcast([P, width // 2, PACK, 2])
             nc.vector.tensor_tensor(
                 grouped.rearrange("p (c e t) -> p c t e", e=2, t=PACK),
                 act.rearrange("p t (c e) -> p c t e", e=2),
@@ -231,8 +216,8 @@ def tile_list_rvq_gelu_mix_gelu_kernel(
                     nc.scalar.activation(rows[:, t, :], act[:, t, :], COPY, scale=factor)
             return rows
 
-        def interleave(grouped, rows, copy=nc.vector.tensor_copy):
-            copy(
+        def interleave(grouped, rows):
+            nc.vector.tensor_copy(
                 grouped.rearrange("p (c e t) -> p c t e", e=PACK, t=PACK),
                 rows.rearrange("p t (c e) -> p c t e", e=PACK),
             )
@@ -246,14 +231,15 @@ def tile_list_rvq_gelu_mix_gelu_kernel(
         def second_layer(banks, h8, h4, cols, j_first, name):
             width = cols.stop - cols.start
             step = HALF if width == HALF else P
-            for n in range(2):
-                y = bank(banks[n], width)
+            sums = [bank(banks[n], width) for n in range(2)]
+            for n, y in enumerate(sums):
                 nc.tensor.matmul_mx(
                     y, lhsT=wd8_w[:, n * P : (n + 1) * P].bitcast(FP8X4),
                     lhsT_scale=wd8_s[:, n * P : (n + 1) * P],
                     rhs=h8[0][:, cols].bitcast(FP8X4), rhs_scale=h8[1][:, cols],
                     start=True, stop=False,
                 )
+            for n, y in enumerate(sums):
                 for c in range(0, width, step):
                     part = slice(cols.start + c, cols.start + c + step)
                     nc.tensor.matmul_mx(
@@ -266,6 +252,12 @@ def tile_list_rvq_gelu_mix_gelu_kernel(
                 nc.scalar.activation(result[:], y, GELU, bias=b_sb[:, n : n + 1])
                 nc.sync.dma_start(out[n * P : (n + 1) * P, j_first + cols.start : j_first + cols.stop], result[:])
 
+        for c in range(WARM_UPS):
+            nc.tensor.matmul_mx(
+                bank(7, HALF), lhsT=w_codes[1, 0, 0], lhsT_scale=v_s[1, 0][:, :P],
+                rhs=tab_w[:, c * HALF : (c + 1) * HALF].bitcast(FP8X4), rhs_scale=tab_s[:, c * HALF : (c + 1) * HALF],
+                start=True, stop=True,
+            )
         acc = [[bank(PACK * u + t, HALF) for t in range(PACK)] for u in range(2)]
         first_layer(acc, 0)
         act0 = activate(acc[0], placed([P, PACK, HALF], F32, "act00", ACT0), PACK)
@@ -273,42 +265,40 @@ def tile_list_rvq_gelu_mix_gelu_kernel(
         gather_words(2, 1, late[:, 0])
         gather_words(0, 1, late[:, 1])
         act1 = activate(acc[1], kept([P, PACK, HALF], F32, "act10"))
-        rows = [smooth_rows(act0[:], 0, PACK, placed([P, PACK, HALF], BF16, "smoothed00", W2S_RAW + 512)),
-                smooth_rows(act1[:], 1, 3, placed([P, PACK, HALF], BF16, "smoothed10", ROWS))]
+        rows = [smooth_rows(act0[:], 0, PACK, placed([P, PACK, HALF], BF16, "smoothed00", W2S_RAW + KB)),
+                smooth_rows(act1[:], 1, 2, placed([P, PACK, HALF], BF16, "smoothed10", ROWS))]
         grouped = [kept([P, HALF * PACK], BF16, f"h0{u}") for u in range(2)]
         h_first = [h_tiles(f"0{u}") for u in range(2)]
-        interleave(grouped[0][:, : SCALAR_SHARE * PACK], rows[0][:, :, :SCALAR_SHARE], nc.scalar.copy)
-        interleave(grouped[0][:, SCALAR_SHARE * PACK :], rows[0][:, :, SCALAR_SHARE:])
+        nc.gpsimd.tensor_copy(
+            grouped[0][:, : GPSIMD_SHARE * PACK].rearrange("p (c t) -> p c t", t=PACK),
+            rows[0][:, :, :GPSIMD_SHARE].rearrange("p t c -> p c t"),
+        )
         interleave(grouped[1][:], rows[1][:])
-        for u in range(2):
+        interleave(grouped[0][:, GPSIMD_SHARE * PACK :], rows[0][:, :, GPSIMD_SHARE:])
+        for u in (1, 0):
             quantise_h(h_first[u], slice(0, HALF), grouped[u][:])
 
         acc = [[bank(PACK * u + t, HALF) for t in range(PACK)] for u in range(2)]
         first_layer(acc, 1)
         act0 = activate(acc[0], kept([P, PACK, HALF], F32, "act01"))
-        sm_bank = bank(2, P)
-        nc.tensor.transpose(sm_bank, sm_rows[:], identity[:])
         act1 = activate(acc[1], kept([P, PACK, HALF], F32, "act11"))
+        rows = smooth_rows(act1[:, :, QUARTER:], 1, 0, kept([P, PACK, QUARTER], BF16, "smoothed1"))
+
         h8, h4 = h_tiles("10"), h_tiles("11")
+        pieces = [(0, slice(0, QUARTER)), (0, slice(QUARTER, HALF)), (1, slice(0, QUARTER)),
+                  (1, slice(QUARTER, QUARTER + P)), (1, slice(QUARTER + P, HALF))]
         h_second = placed([P, 2, HALF * PACK], BF16, "h1", ROWS)
-
-        def grouped_cols(u, cols):
-            return h_second[:, u, cols.start * PACK : cols.stop * PACK]
-
-        first, rest = slice(0, QUARTER), slice(QUARTER, HALF)
-        third, last = slice(QUARTER, QUARTER + P), slice(QUARTER + P, HALF)
-        smooth_on_vector(grouped_cols(0, first), act0[:, :, first], sm_bank[:, :PACK])
-        rows = smooth_rows(act0[:, :, rest], 0, PACK, kept([P, PACK, QUARTER], BF16, "smoothed01"))
-        interleave(grouped_cols(0, rest), rows[:])
-        quantise_h(h8, first, grouped_cols(0, first))
-        quantise_h(h8, rest, grouped_cols(0, rest))
-        smooth_on_vector(grouped_cols(1, first), act1[:, :, first], sm_bank[:, PACK : 2 * PACK])
-        pieces = [first, third, last]
-        for before, cols, rows_on_gpsimd in ((first, third, PACK), (third, last, 0)):
-            rows = smooth_rows(act1[:, :, cols], 1, rows_on_gpsimd, kept([P, PACK, P], BF16, f"smoothed1{cols.start}"))
-            interleave(grouped_cols(1, cols), rows[:])
-            quantise_h(h4, before, grouped_cols(1, before))
-        quantise_h(h4, last, grouped_cols(1, last))
+        waiting = None
+        for u, cols in pieces:
+            grouped = h_second[:, u, cols.start * PACK : cols.stop * PACK]
+            if u == 0 or cols.start == 0:
+                smooth_on_vector(grouped, (act0, act1)[u][:, :, cols], u)
+            else:
+                interleave(grouped, rows[:, :, cols.start - QUARTER : cols.stop - QUARTER])
+            if waiting:
+                quantise_h(*waiting)
+            waiting = ((h8, h4)[u], cols, grouped)
+        quantise_h(*waiting)
         second_layer((0, 1), h_first[0], h_first[1], slice(0, HALF), 0, "0")
-        for c, (cols, banks) in enumerate(zip(pieces, ((3, 4), (5, 6), (7, 0)))):
-            second_layer(banks, h8, h4, cols, HALF, f"1{c}")
+        for c, (u, cols) in enumerate(pieces[2:]):
+            second_layer((2 + 2 * c, 3 + 2 * c), h8, h4, cols, HALF, f"1{c}")

@@ -23,7 +23,6 @@ PACK = 4
 HALF = 512
 QUARTER = 256
 KB = 1024
-GPSIMD_SHARE = 256
 WARM_UPS = 3
 
 
@@ -266,16 +265,12 @@ def tile_list_rvq_gelu_mix_gelu_kernel(
         gather_words(0, 1, late[:, 1])
         act1 = activate(acc[1], kept([P, PACK, HALF], F32, "act10"))
         rows = [smooth_rows(act0[:], 0, PACK, placed([P, PACK, HALF], BF16, "smoothed00", W2S_RAW + KB)),
-                smooth_rows(act1[:], 1, 2, placed([P, PACK, HALF], BF16, "smoothed10", ROWS))]
+                smooth_rows(act1[:], 1, 1, placed([P, PACK, HALF], BF16, "smoothed10", ROWS))]
         grouped = [kept([P, HALF * PACK], BF16, f"h0{u}") for u in range(2)]
         h_first = [h_tiles(f"0{u}") for u in range(2)]
-        nc.gpsimd.tensor_copy(
-            grouped[0][:, : GPSIMD_SHARE * PACK].rearrange("p (c t) -> p c t", t=PACK),
-            rows[0][:, :, :GPSIMD_SHARE].rearrange("p t c -> p c t"),
-        )
-        interleave(grouped[1][:], rows[1][:])
-        interleave(grouped[0][:, GPSIMD_SHARE * PACK :], rows[0][:, :, GPSIMD_SHARE:])
-        for u in (1, 0):
+        for u in range(2):
+            interleave(grouped[u][:], rows[u][:])
+        for u in range(2):
             quantise_h(h_first[u], slice(0, HALF), grouped[u][:])
 
         acc = [[bank(PACK * u + t, HALF) for t in range(PACK)] for u in range(2)]

@@ -23,7 +23,6 @@ PACK = 4
 HALF = 512
 QUARTER = 256
 KB = 1024
-WARM_UPS = 3
 
 
 def tile_list_rvq_gelu_mix_gelu_kernel(
@@ -251,12 +250,6 @@ def tile_list_rvq_gelu_mix_gelu_kernel(
                 nc.scalar.activation(result[:], y, GELU, bias=b_sb[:, n : n + 1])
                 nc.sync.dma_start(out[n * P : (n + 1) * P, j_first + cols.start : j_first + cols.stop], result[:])
 
-        for c in range(WARM_UPS):
-            nc.tensor.matmul_mx(
-                bank(7, HALF), lhsT=w_codes[1, 0, 0], lhsT_scale=v_s[1, 0][:, :P],
-                rhs=tab_w[:, c * HALF : (c + 1) * HALF].bitcast(FP8X4), rhs_scale=tab_s[:, c * HALF : (c + 1) * HALF],
-                start=True, stop=True,
-            )
         acc = [[bank(PACK * u + t, HALF) for t in range(PACK)] for u in range(2)]
         first_layer(acc, 0)
         act0 = activate(acc[0], placed([P, PACK, HALF], F32, "act00", ACT0), PACK)

@@ -42,10 +42,8 @@ def tile_list_rvq_gelu_mix_gelu_kernel(
             return reused.tile(shape, dtype, name=name, offset=offset, align_bytes=64)
 
         def load_scale_rows(scales, plane):
-            for q in range(4):
-                nc.sync.dma_start(
-                    plane[32 * q : 32 * q + 4, :].bitcast(I32), scales[0, 4 * q : 4 * q + 4, :].bitcast(I32)
-                )
+            for r in range(4):
+                nc.sync.dma_start(plane[r:P:32, :].bitcast(I32), scales[0, r:16:4, :].bitcast(I32))
 
         W0_LOW, ACT0, W0_HIGH = 0, 8 * KB, 15 * KB
         GROUPED, W2S_RAW, ROWS, NO_BIAS = 23 * KB, 27 * KB, 32 * KB, 40 * KB

@@ -63,7 +63,7 @@ def tile_list_rvq_gelu_mix_gelu_kernel(
         w1s_raw = kept([P, R], U8, "w1s_raw")
         nc.vector.memset(w1s_raw[:].bitcast(I32), 0)
         load_scale_rows(w1_scales, w1s_raw[:])
-        w2s_raw = placed([P, R], U8, "w2s_raw", W2S_RAW)
+        w2s_raw = kept([P, R], U8, "w2s_raw")
         nc.vector.memset(w2s_raw[:].bitcast(I32), 0)
         wd_s = kept([P, 2 * N], U8, "wd_s")
         nc.vector.memset(wd_s[:].bitcast(I32), 0)
@@ -150,7 +150,7 @@ def tile_list_rvq_gelu_mix_gelu_kernel(
         for g, raw in ((1, w1_raw), (2, w2_raw)):
             for u in range(2):
                 deal_words(g, u, raw)
-        for g, u, raw in ((1, 0, w1s_raw), (2, 0, w2s_raw), (2, 1, w2s_raw)):
+        for g, u, raw in ((1, 0, w1s_raw), (1, 1, w1s_raw), (2, 0, w2s_raw)):
             deal_scales(g, u, raw, kept([P, HALF], U8, f"w{g}_scales{u}"))
         early = kept([P, 3 * HALF], U8, "picked_s_early")
         nc.vector.tensor_copy(early[:], tab_s[:].indirect(offsets[:, J // 16 : (J + 3 * HALF) // 16]))
@@ -163,7 +163,7 @@ def tile_list_rvq_gelu_mix_gelu_kernel(
         grouped_low = round_w0(w0_low, placed([P, HALF * PACK], BF16, "w0_grouped0", GROUPED))
         grouped_high = round_w0(w0_high, placed([P, HALF * PACK], BF16, "w0_grouped1", W2S_RAW + KB))
         quantise_w0(0, grouped_low)
-        deal_scales(1, 1, w1s_raw, placed([P, HALF], U8, "w1_scales1", W2S_RAW - 256))
+        deal_scales(2, 1, w2s_raw, placed([P, HALF], U8, "w2_scales1", GROUPED))
         gather_words(1, 1, placed([P, HALF], U32, "picked_w1_1", W0_LOW)[:])
         quantise_w0(1, grouped_high)
         gather_scales(2, 1, W0_HIGH + KB + HALF)
@@ -177,7 +177,7 @@ def tile_list_rvq_gelu_mix_gelu_kernel(
             nc.tensor.matmul_mx(
                 acc[u][t], lhsT=w_codes[g, u, t], lhsT_scale=w_scales[g, u, t],
                 rhs=v_w[g, half].bitcast(FP8X4), rhs_scale=v_s[g, half],
-                start=(g == 1), stop=(g == 0),
+                start=(g == 1 + u), stop=(g == 0),
             )
 
         def first_layer(acc, half):
@@ -185,7 +185,7 @@ def tile_list_rvq_gelu_mix_gelu_kernel(
                 for t in range(PACK):
                     first_layer_pass(acc, g, 0, t, half)
             for t in range(PACK):
-                for g in (1, 2, 0):
+                for g in (2, 1, 0):
                     first_layer_pass(acc, g, 1, t, half)
 
         def activate(acc, act, with_bias_tile=0):
@@ -285,6 +285,6 @@ def tile_list_rvq_gelu_mix_gelu_kernel(
                 quantise_h(*waiting)
             waiting = ((h8, h4)[u], cols, grouped)
         quantise_h(*waiting)
-        second_layer((0, 1), h_first[0], h_first[1], slice(0, HALF), 0, "0")
+        second_layer((0, 7), h_first[0], h_first[1], slice(0, HALF), 0, "0")
         for c, (u, cols) in enumerate(pieces[2:]):
-            second_layer((2 + 2 * c, 3 + 2 * c), h8, h4, cols, HALF, f"1{c}")
+            second_layer((1 + 2 * c, 2 + 2 * c), h8, h4, cols, HALF, f"1{c}")

@@ -54,15 +54,17 @@ def tile_list_rvq_gelu_mix_gelu_kernel(
         nc.vector.memset(tab_s[:].bitcast(I32), 0)
         load_scale_rows(tab_scales, tab_s[:])
         w1_raw = kept([P, 2 * R], U8, "w1_raw")
-        nc.sync.dma_start(w1_raw[:].bitcast(I32), w1_words[0].bitcast(I32))
-        w2_raw = kept([P, 2 * R], U8, "w2_raw")
-        nc.sync.dma_start(w2_raw[:].bitcast(I32), w2_words[0].bitcast(I32))
+        for u in range(2):
+            cols = slice(2 * u * HALF, 2 * (u + 1) * HALF)
+            nc.sync.dma_start(w1_raw[:, cols].bitcast(I32), w1_words[0, :, cols].bitcast(I32))
         tab_w = kept([P, T], I32, "tab_w")
         nc.sync.dma_start(tab_w[:], tab_words[0].rearrange("p t i -> p (t i)").bitcast(I32))
 
         w1s_raw = kept([P, R], U8, "w1s_raw")
         nc.vector.memset(w1s_raw[:].bitcast(I32), 0)
         load_scale_rows(w1_scales, w1s_raw[:])
+        w2_raw = placed([P, 2 * R], U8, "w2_raw", GROUPED)
+        nc.sync.dma_start(w2_raw[:].bitcast(I32), w2_words[0].bitcast(I32))
         w2s_raw = kept([P, R], U8, "w2s_raw")
         nc.vector.memset(w2s_raw[:].bitcast(I32), 0)
         wd_s = kept([P, 2 * N], U8, "wd_s")
@@ -91,9 +93,9 @@ def tile_list_rvq_gelu_mix_gelu_kernel(
 
         def deal_words(g, u, raw):
             codes = kept([P, 2 * HALF], U8, f"w{g}_codes{u}")
-            nc.gpsimd.tensor_copy(
-                codes[:].rearrange("p (t m e) -> p t m e", t=PACK, e=2),
-                raw[:, 2 * u * HALF : 2 * (u + 1) * HALF].rearrange("p (m t e) -> p t m e", t=PACK, e=2),
+            nc.scalar.copy(
+                codes[:].bitcast(U16).rearrange("p (t m) -> p t m", t=PACK),
+                raw[:, 2 * u * HALF : 2 * (u + 1) * HALF].bitcast(U16).rearrange("p (m t) -> p t m", t=PACK),
             )
             for t in range(PACK):
                 w_codes[g, u, t] = codes[:, 2 * t * P : 2 * (t + 1) * P].bitcast(FP4X4)

@@ -159,8 +159,12 @@ def tile_list_rvq_gelu_mix_gelu_kernel(
         for c, place in enumerate(((1, 0), (1, 1), (2, 0))):
             v_s[place] = early[:, c * HALF : (c + 1) * HALF]
         gather_scales(0, 0)
-        for g in (1, 2, 0):
+        for g in (1, 0):
             gather_words(g, 0, kept([P, HALF], U32, f"picked_w{g}_0")[:])
+        both = kept([P, J], U32, "picked_w2")
+        nc.vector.tensor_copy(both[:], tab_w[:].bitcast(U32).indirect(offsets[:, 2 * J // 16 :]))
+        for half in range(2):
+            v_w[2, half] = both[:, half * HALF : (half + 1) * HALF]
 
         grouped_low = round_w0(w0_low, placed([P, HALF * PACK], BF16, "w0_grouped0", GROUPED))
         grouped_high = round_w0(w0_high, placed([P, HALF * PACK], BF16, "w0_grouped1", W2S_RAW + KB))
@@ -179,15 +183,16 @@ def tile_list_rvq_gelu_mix_gelu_kernel(
             nc.tensor.matmul_mx(
                 acc[u][t], lhsT=w_codes[g, u, t], lhsT_scale=w_scales[g, u, t],
                 rhs=v_w[g, half].bitcast(FP8X4), rhs_scale=v_s[g, half],
-                start=(g == 1 + u), stop=(g == 0),
+                start=(g == 1), stop=(g == 0),
             )
 
         def first_layer(acc, half):
-            for g in (1, 2, 0):
+            early = half == 0
+            for g, u in ((1, 0), (1, 1), (2, 0), (0, 0)) if early else ((1, 0), (2, 0), (0, 0)):
                 for t in range(PACK):
-                    first_layer_pass(acc, g, 0, t, half)
+                    first_layer_pass(acc, g, u, t, half)
             for t in range(PACK):
-                for g in (2, 1, 0):
+                for g in (2, 0) if early else (1, 2, 0):
                     first_layer_pass(acc, g, 1, t, half)
 
         def activate(acc, act, with_bias_tile=0):
@@ -253,16 +258,15 @@ def tile_list_rvq_gelu_mix_gelu_kernel(
         acc = [[bank(PACK * u + t, HALF) for t in range(PACK)] for u in range(2)]
         first_layer(acc, 0)
         act0 = activate(acc[0], placed([P, PACK, HALF], F32, "act00", ACT0), PACK)
-        late = placed([P, 2, HALF], U32, "picked_late", NO_BIAS)
-        gather_words(2, 1, late[:, 0])
-        gather_words(0, 1, late[:, 1])
+        gather_words(0, 1, placed([P, HALF], U32, "picked_late", NO_BIAS)[:])
         act1 = activate(acc[1], kept([P, PACK, HALF], F32, "act10"))
         rows = [smooth_rows(act0[:], 0, PACK, placed([P, PACK, HALF], BF16, "smoothed00", W2S_RAW + KB)),
-                smooth_rows(act1[:], 1, 1, placed([P, PACK, HALF], BF16, "smoothed10", ROWS))]
-        grouped = [kept([P, HALF * PACK], BF16, f"h0{u}") for u in range(2)]
+                smooth_rows(act1[:, :, :QUARTER], 1, 0, placed([P, PACK, QUARTER], BF16, "smoothed10", ROWS))]
+        grouped = [kept([P, HALF * PACK], BF16, "h00"), placed([P, HALF * PACK], BF16, "h01", ACT0)]
         h_first = [h_tiles(f"0{u}") for u in range(2)]
-        for u in range(2):
-            interleave(grouped[u][:], rows[u][:])
+        interleave(grouped[0][:], rows[0][:])
+        smooth_on_vector(grouped[1][:, QUARTER * PACK :], act1[:, :, QUARTER:], 1)
+        interleave(grouped[1][:, : QUARTER * PACK], rows[1][:])
         for u in range(2):
             quantise_h(h_first[u], slice(0, HALF), grouped[u][:])
 
@@ -270,11 +274,12 @@ def tile_list_rvq_gelu_mix_gelu_kernel(
         first_layer(acc, 1)
         act0 = activate(acc[0], kept([P, PACK, HALF], F32, "act01"))
         act1 = activate(acc[1], kept([P, PACK, HALF], F32, "act11"))
-        rows = smooth_rows(act1[:, :, QUARTER:], 1, 0, kept([P, PACK, QUARTER], BF16, "smoothed1"))
+        rows = {cols.start: smooth_rows(act1[:, :, cols], 1, 0, kept([P, PACK, cols.stop - cols.start], BF16, f"smoothed1{cols.start}"))
+                for cols in (slice(P, HALF - P), slice(HALF - P, HALF))}
 
         h8, h4 = h_tiles("10"), h_tiles("11")
-        pieces = [(0, slice(0, QUARTER)), (0, slice(QUARTER, HALF)), (1, slice(0, QUARTER)),
-                  (1, slice(QUARTER, QUARTER + P)), (1, slice(QUARTER + P, HALF))]
+        pieces = [(0, slice(0, QUARTER)), (0, slice(QUARTER, HALF)), (1, slice(0, P)),
+                  (1, slice(P, HALF - P)), (1, slice(HALF - P, HALF))]
         h_second = placed([P, 2, HALF * PACK], BF16, "h1", ROWS)
         waiting = None
         for u, cols in pieces:
@@ -282,7 +287,7 @@ def tile_list_rvq_gelu_mix_gelu_kernel(
             if u == 0 or cols.start == 0:
                 smooth_on_vector(grouped, (act0, act1)[u][:, :, cols], u)
             else:
-                interleave(grouped, rows[:, :, cols.start - QUARTER : cols.stop - QUARTER])
+                interleave(grouped, rows[cols.start][:])
             if waiting:
                 quantise_h(*waiting)
             waiting = ((h8, h4)[u], cols, grouped)

@@ -47,6 +47,8 @@ def tile_list_rvq_gelu_mix_gelu_kernel(
 
         W0_LOW, ACT0, W0_HIGH = 0, 8 * KB, 15 * KB
         GROUPED, W2S_RAW, ROWS, NO_BIAS = 23 * KB, 27 * KB, 32 * KB, 40 * KB
+        WARM_UPS = 4
+        SM_WIDE = 44 * KB
 
         offsets = keep.tile([P, 3 * J // 16], U16, name="offsets")
         nc.sync.dma_start(offsets[:], offs)
@@ -74,6 +76,12 @@ def tile_list_rvq_gelu_mix_gelu_kernel(
         nc.vector.memset(zero[:], 0.0)
         no_bias = placed([P, 1], F32, "no_bias", NO_BIAS)
         nc.scalar.activation(no_bias[:], zero[:], GELU)
+
+        zeros = kept([P, QUARTER * PACK], BF16, "zeros")
+        nc.vector.memset(zeros[:].bitcast(I32), 0)
+        zero_codes = kept([P, QUARTER], U32, "zero_codes")
+        zero_scales = kept([P, QUARTER], U8, "zero_scales")
+        nc.vector.quantize_mx(zero_codes[:].bitcast(FP8X4), zero_scales[:], zeros[:])
 
         def offsets_of(g, half):
             first = (g * J + half * HALF) // 16
@@ -121,8 +129,7 @@ def tile_list_rvq_gelu_mix_gelu_kernel(
             dealt = grouped[:].rearrange("p (a e m i) -> p a m i e", a=2, e=2, i=PACK)
             for c in range(2):
                 src = raw[:, c].rearrange("p i (m a e) -> p a m i e", a=2, e=2)
-                for a in range(2):
-                    nc.scalar.copy(dealt[:, a, c * 64 : (c + 1) * 64], src[:, a])
+                nc.scalar.copy(dealt[:, :, c * 64 : (c + 1) * 64], src)
             return grouped
 
         def quantise_w0(u, grouped):
@@ -140,6 +147,8 @@ def tile_list_rvq_gelu_mix_gelu_kernel(
         nc.sync.dma_start(wd8_w[:], wd8_words[0].rearrange("p n i -> p (n i)").bitcast(I32))
         sm_sb = kept([P, 2, PACK], F32, "sm_sb")
         nc.sync.dma_start(sm_sb[:], sm.rearrange("(u p t) -> p u t", u=2, t=PACK))
+        sm_wide = placed([P, PACK], F32, "sm_wide", SM_WIDE)
+        nc.gpsimd.tensor_copy(sm_wide[:], sm_sb[:, 1, :])
         wd4_w = kept([P, 2 * N], U8, "wd4_w")
         nc.sync.dma_start(wd4_w[:].bitcast(I32), wd4_words[0].bitcast(I32))
         wd8_s, wd4_s = wd_s[:, :N], wd_s[:, N:]
@@ -159,12 +168,12 @@ def tile_list_rvq_gelu_mix_gelu_kernel(
         for c, place in enumerate(((1, 0), (1, 1), (2, 0))):
             v_s[place] = early[:, c * HALF : (c + 1) * HALF]
         gather_scales(0, 0)
-        for g in (1, 0):
-            gather_words(g, 0, kept([P, HALF], U32, f"picked_w{g}_0")[:])
+        gather_words(1, 0, kept([P, HALF], U32, "picked_w1_0")[:])
         both = kept([P, J], U32, "picked_w2")
         nc.vector.tensor_copy(both[:], tab_w[:].bitcast(U32).indirect(offsets[:, 2 * J // 16 :]))
         for half in range(2):
             v_w[2, half] = both[:, half * HALF : (half + 1) * HALF]
+        gather_words(0, 0, kept([P, HALF], U32, "picked_w0_0")[:])
 
         grouped_low = round_w0(w0_low, placed([P, HALF * PACK], BF16, "w0_grouped0", GROUPED))
         grouped_high = round_w0(w0_high, placed([P, HALF * PACK], BF16, "w0_grouped1", W2S_RAW + KB))
@@ -255,6 +264,13 @@ def tile_list_rvq_gelu_mix_gelu_kernel(
                 nc.scalar.activation(result[:], y, GELU, bias=b_sb[:, n : n + 1])
                 nc.sync.dma_start(out[n * P : (n + 1) * P, j_first + cols.start : j_first + cols.stop], result[:])
 
+        idle = bank(2 * PACK - 1, QUARTER)
+        for repeat in range(WARM_UPS):
+            nc.tensor.matmul_mx(
+                idle, lhsT=w_codes[1, 0, 0], lhsT_scale=w1s_raw[:, :P],
+                rhs=zero_codes[:].bitcast(FP8X4), rhs_scale=zero_scales[:], start=True, stop=True,
+            )
+
         acc = [[bank(PACK * u + t, HALF) for t in range(PACK)] for u in range(2)]
         first_layer(acc, 0)
         act0 = activate(acc[0], placed([P, PACK, HALF], F32, "act00", ACT0), PACK)
@@ -274,24 +290,29 @@ def tile_list_rvq_gelu_mix_gelu_kernel(
         first_layer(acc, 1)
         act0 = activate(acc[0], kept([P, PACK, HALF], F32, "act01"))
         act1 = activate(acc[1], kept([P, PACK, HALF], F32, "act11"))
-        rows = {cols.start: smooth_rows(act1[:, :, cols], 1, 0, kept([P, PACK, cols.stop - cols.start], BF16, f"smoothed1{cols.start}"))
-                for cols in (slice(P, HALF - P), slice(HALF - P, HALF))}
+        rows = [kept([P, PACK, QUARTER], BF16, "smoothed_wide"), kept([P, PACK, P], BF16, "smoothed_last")]
+        for t in range(PACK):
+            nc.scalar.activation(rows[0][:, t, :], act1[:, t, P : HALF - P], COPY, scale=sm_wide[:, t : t + 1])
+        smooth_rows(act1[:, :, HALF - P :], 1, 0, rows[1])
 
+        pieces = [slice(0, QUARTER), slice(QUARTER, HALF - P), slice(HALF - P, HALF)]
         h8, h4 = h_tiles("10"), h_tiles("11")
-        pieces = [(0, slice(0, QUARTER)), (0, slice(QUARTER, HALF)), (1, slice(0, P)),
-                  (1, slice(P, HALF - P)), (1, slice(HALF - P, HALF))]
+        later8 = (kept([P, HALF], U32, "h_codes_later"), placed([P, HALF], U8, "h_scales_later", SM_WIDE))
         h_second = placed([P, 2, HALF * PACK], BF16, "h1", ROWS)
-        waiting = None
-        for u, cols in pieces:
-            grouped = h_second[:, u, cols.start * PACK : cols.stop * PACK]
-            if u == 0 or cols.start == 0:
-                smooth_on_vector(grouped, (act0, act1)[u][:, :, cols], u)
-            else:
-                interleave(grouped, rows[cols.start][:])
-            if waiting:
-                quantise_h(*waiting)
-            waiting = ((h8, h4)[u], cols, grouped)
-        quantise_h(*waiting)
+
+        def columns(u, cols):
+            return h_second[:, u, cols.start * PACK : cols.stop * PACK]
+
+        for cols in (slice(0, QUARTER), slice(QUARTER, HALF)):
+            smooth_on_vector(columns(0, cols), act0[:, :, cols], 0)
+        quantise_h(h8, pieces[0], columns(0, pieces[0]))
+        smooth_on_vector(columns(1, slice(0, P)), act1[:, :, :P], 1)
+        interleave(columns(1, slice(P, HALF - P)), rows[0][:])
+        quantise_h(later8, slice(QUARTER, HALF), columns(0, slice(QUARTER, HALF)))
+        quantise_h(h4, pieces[0], columns(1, pieces[0]))
+        interleave(columns(1, pieces[2]), rows[1][:])
+        for cols in pieces[1:]:
+            quantise_h(h4, cols, columns(1, cols))
         second_layer((0, 7), h_first[0], h_first[1], slice(0, HALF), 0, "0")
-        for c, (u, cols) in enumerate(pieces[2:]):
-            second_layer((1 + 2 * c, 2 + 2 * c), h8, h4, cols, HALF, f"1{c}")
+        for c, cols in enumerate(pieces):
+            second_layer((1 + 2 * c, 2 + 2 * c), later8 if c else h8, h4, cols, HALF, f"1{c}")

@@ -1,6 +1,7 @@
 from contextlib import ExitStack
 
 import concourse.mybir as mybir
+from concourse.masks import make_identity
 
 K, R, N, T, J = 512, 1024, 256, 4096, 1024
 FLOPS = 2 * (3 * K * R * J + R * N * J)
@@ -47,7 +48,6 @@ def tile_list_rvq_gelu_mix_gelu_kernel(
 
         W0_LOW, ACT0, W0_HIGH = 0, 8 * KB, 15 * KB
         GROUPED, W2S_RAW, ROWS, NO_BIAS = 23 * KB, 27 * KB, 32 * KB, 40 * KB
-        WARM_UPS = 4
         SM_WIDE = 44 * KB
 
         offsets = keep.tile([P, 3 * J // 16], U16, name="offsets")
@@ -55,10 +55,10 @@ def tile_list_rvq_gelu_mix_gelu_kernel(
         tab_s = kept([P, T], U8, "tab_s")
         nc.vector.memset(tab_s[:].bitcast(I32), 0)
         load_scale_rows(tab_scales, tab_s[:])
+        sm_sb = kept([P, 2, PACK], F32, "sm_sb")
+        nc.sync.dma_start(sm_sb[:], sm.rearrange("(u p t) -> p u t", u=2, t=PACK))
         w1_raw = kept([P, 2 * R], U8, "w1_raw")
-        for u in range(2):
-            cols = slice(2 * u * HALF, 2 * (u + 1) * HALF)
-            nc.sync.dma_start(w1_raw[:, cols].bitcast(I32), w1_words[0, :, cols].bitcast(I32))
+        nc.sync.dma_start(w1_raw[:].bitcast(I32), w1_words[0].bitcast(I32))
         tab_w = kept([P, T], I32, "tab_w")
         nc.sync.dma_start(tab_w[:], tab_words[0].rearrange("p t i -> p (t i)").bitcast(I32))
 
@@ -72,16 +72,19 @@ def tile_list_rvq_gelu_mix_gelu_kernel(
         wd_s = kept([P, 2 * N], U8, "wd_s")
         nc.vector.memset(wd_s[:].bitcast(I32), 0)
 
+        sm_twice = kept([P, P], F32, "sm_twice")
+        nc.vector.memset(sm_twice[:], 0.0)
+        identity = kept([P, P], F32, "identity")
+        nc.vector.memset(identity[:], 0.0)
+        make_identity(nc, identity[:], nomemset=True)
+        nc.gpsimd.tensor_copy(
+            sm_twice[:, : 4 * PACK].rearrange("p (c e) -> p c e", e=2),
+            sm_sb[:].rearrange("p u t -> p (u t)").unsqueeze(2).to_broadcast([P, 2 * PACK, 2]),
+        )
         zero = kept([P, 1], F32, "zero")
         nc.vector.memset(zero[:], 0.0)
         no_bias = placed([P, 1], F32, "no_bias", NO_BIAS)
         nc.scalar.activation(no_bias[:], zero[:], GELU)
-
-        zeros = kept([P, QUARTER * PACK], BF16, "zeros")
-        nc.vector.memset(zeros[:].bitcast(I32), 0)
-        zero_codes = kept([P, QUARTER], U32, "zero_codes")
-        zero_scales = kept([P, QUARTER], U8, "zero_scales")
-        nc.vector.quantize_mx(zero_codes[:].bitcast(FP8X4), zero_scales[:], zeros[:])
 
         def offsets_of(g, half):
             first = (g * J + half * HALF) // 16
@@ -145,10 +148,10 @@ def tile_list_rvq_gelu_mix_gelu_kernel(
         w0_high = load_w0(1, W0_HIGH)
         wd8_w = kept([P, N], I32, "wd8_w")
         nc.sync.dma_start(wd8_w[:], wd8_words[0].rearrange("p n i -> p (n i)").bitcast(I32))
-        sm_sb = kept([P, 2, PACK], F32, "sm_sb")
-        nc.sync.dma_start(sm_sb[:], sm.rearrange("(u p t) -> p u t", u=2, t=PACK))
         sm_wide = placed([P, PACK], F32, "sm_wide", SM_WIDE)
         nc.gpsimd.tensor_copy(sm_wide[:], sm_sb[:, 1, :])
+        sm_middle = placed([P, PACK], F32, "sm_middle", SM_WIDE + KB)
+        nc.gpsimd.tensor_copy(sm_middle[:], sm_sb[:, 1, :])
         wd4_w = kept([P, 2 * N], U8, "wd4_w")
         nc.sync.dma_start(wd4_w[:].bitcast(I32), wd4_words[0].bitcast(I32))
         wd8_s, wd4_s = wd_s[:, :N], wd_s[:, N:]
@@ -175,6 +178,17 @@ def tile_list_rvq_gelu_mix_gelu_kernel(
             v_w[2, half] = both[:, half * HALF : (half + 1) * HALF]
         gather_words(0, 0, kept([P, HALF], U32, "picked_w0_0")[:])
 
+        def bank(index, width):
+            tile = psum.tile([P, HALF], F32, name="bank", tag=f"bank{index}")
+            return tile[:, :width]
+
+        turned = bank(6, P)
+        nc.tensor.transpose(turned, sm_twice[:], identity[:])
+        sm_turned = placed([P, P], F32, "sm_turned", GROUPED + 2 * KB)
+        nc.scalar.copy(sm_turned[:], turned)
+        sm_psum = bank(7, P)
+        nc.tensor.transpose(sm_psum, sm_turned[:], identity[:])
+
         grouped_low = round_w0(w0_low, placed([P, HALF * PACK], BF16, "w0_grouped0", GROUPED))
         grouped_high = round_w0(w0_high, placed([P, HALF * PACK], BF16, "w0_grouped1", W2S_RAW + KB))
         quantise_w0(0, grouped_low)
@@ -183,10 +197,6 @@ def tile_list_rvq_gelu_mix_gelu_kernel(
         quantise_w0(1, grouped_high)
         gather_scales(2, 1, W0_HIGH + KB + HALF)
         gather_scales(0, 1, W0_HIGH + KB)
-
-        def bank(index, width):
-            tile = psum.tile([P, HALF], F32, name="bank", tag=f"bank{index}")
-            return tile[:, :width]
 
         def first_layer_pass(acc, g, u, t, half):
             nc.tensor.matmul_mx(
@@ -198,20 +208,26 @@ def tile_list_rvq_gelu_mix_gelu_kernel(
         def first_layer(acc, half):
             early = half == 0
             for g, u in ((1, 0), (1, 1), (2, 0), (0, 0)) if early else ((1, 0), (2, 0), (0, 0)):
-                for t in range(PACK):
+                for t in range(len(acc[u])):
                     first_layer_pass(acc, g, u, t, half)
-            for t in range(PACK):
+            for t in range(PACK - 1):
                 for g in (2, 0) if early else (1, 2, 0):
                     first_layer_pass(acc, g, 1, t, half)
+
+        def last_sum(acc, half, index):
+            acc[1].append(bank(index, HALF))
+            for g in (1, 2, 0):
+                first_layer_pass(acc, g, 1, PACK - 1, half)
 
         def activate(acc, act, with_bias_tile=0):
             for t in range(PACK):
                 nc.scalar.activation(act[:, t, :], acc[t], GELU, bias=no_bias[:] if t < with_bias_tile else 0.0)
             return act
 
-        def smooth_on_vector(grouped, act, u):
+        def smooth_on_vector(grouped, act, u, twice=sm_twice):
             width = act.shape[2]
-            factor = sm_sb[:, u, :].unsqueeze(1).unsqueeze(3).to_broadcast([P, width // 2, PACK, 2])
+            pairs = twice[:, 2 * u * PACK : 2 * (u + 1) * PACK].rearrange("p (t e) -> p t e", e=2)
+            factor = pairs.unsqueeze(1).to_broadcast([P, width // 2, PACK, 2])
             nc.vector.tensor_tensor(
                 grouped.rearrange("p (c e t) -> p c t e", e=2, t=PACK),
                 act.rearrange("p t (c e) -> p c t e", e=2),
@@ -219,9 +235,9 @@ def tile_list_rvq_gelu_mix_gelu_kernel(
                 MULT,
             )
 
-        def smooth_rows(act, u, rows_on_gpsimd, rows):
+        def smooth_rows(act, factors, rows_on_gpsimd, rows):
             for t in range(PACK):
-                factor = sm_sb[:, u, t : t + 1]
+                factor = factors[:, t : t + 1]
                 if t < rows_on_gpsimd:
                     nc.gpsimd.tensor_scalar(rows[:, t, :], act[:, t, :], factor, 0.0, MULT, ADD)
                 else:
@@ -264,36 +280,30 @@ def tile_list_rvq_gelu_mix_gelu_kernel(
                 nc.scalar.activation(result[:], y, GELU, bias=b_sb[:, n : n + 1])
                 nc.sync.dma_start(out[n * P : (n + 1) * P, j_first + cols.start : j_first + cols.stop], result[:])
 
-        idle = bank(2 * PACK - 1, QUARTER)
-        for repeat in range(WARM_UPS):
-            nc.tensor.matmul_mx(
-                idle, lhsT=w_codes[1, 0, 0], lhsT_scale=w1s_raw[:, :P],
-                rhs=zero_codes[:].bitcast(FP8X4), rhs_scale=zero_scales[:], start=True, stop=True,
-            )
-
-        acc = [[bank(PACK * u + t, HALF) for t in range(PACK)] for u in range(2)]
+        acc = [[bank(t, HALF) for t in range(PACK)], [bank(PACK + t, HALF) for t in range(PACK - 1)]]
         first_layer(acc, 0)
         act0 = activate(acc[0], placed([P, PACK, HALF], F32, "act00", ACT0), PACK)
         gather_words(0, 1, placed([P, HALF], U32, "picked_late", NO_BIAS)[:])
+        last_sum(acc, 0, 0)
         act1 = activate(acc[1], kept([P, PACK, HALF], F32, "act10"))
-        rows = [smooth_rows(act0[:], 0, PACK, placed([P, PACK, HALF], BF16, "smoothed00", W2S_RAW + KB)),
-                smooth_rows(act1[:, :, :QUARTER], 1, 0, placed([P, PACK, QUARTER], BF16, "smoothed10", ROWS))]
+        rows = [smooth_rows(act0[:], sm_sb[:, 0, :], PACK, placed([P, PACK, HALF], BF16, "smoothed00", W2S_RAW + KB)),
+                smooth_rows(act1[:, :, :QUARTER], sm_middle, 0, placed([P, PACK, QUARTER], BF16, "smoothed10", ROWS))]
         grouped = [kept([P, HALF * PACK], BF16, "h00"), placed([P, HALF * PACK], BF16, "h01", ACT0)]
-        h_first = [h_tiles(f"0{u}") for u in range(2)]
+        h_first = [(kept([P, HALF], U32, "h_codes00"), placed([P, HALF], U8, "h_scales00", SM_WIDE + KB)), h_tiles("01")]
         interleave(grouped[0][:], rows[0][:])
         smooth_on_vector(grouped[1][:, QUARTER * PACK :], act1[:, :, QUARTER:], 1)
         interleave(grouped[1][:, : QUARTER * PACK], rows[1][:])
         for u in range(2):
             quantise_h(h_first[u], slice(0, HALF), grouped[u][:])
 
-        acc = [[bank(PACK * u + t, HALF) for t in range(PACK)] for u in range(2)]
+        acc = [[bank(1 + t, HALF) for t in range(PACK)], [bank((5 + t) % 7, HALF) for t in range(PACK - 1)]]
         first_layer(acc, 1)
         act0 = activate(acc[0], kept([P, PACK, HALF], F32, "act01"))
+        last_sum(acc, 1, 1)
         act1 = activate(acc[1], kept([P, PACK, HALF], F32, "act11"))
         rows = [kept([P, PACK, QUARTER], BF16, "smoothed_wide"), kept([P, PACK, P], BF16, "smoothed_last")]
-        for t in range(PACK):
-            nc.scalar.activation(rows[0][:, t, :], act1[:, t, P : HALF - P], COPY, scale=sm_wide[:, t : t + 1])
-        smooth_rows(act1[:, :, HALF - P :], 1, 0, rows[1])
+        smooth_rows(act1[:, :, P : HALF - P], sm_wide, 0, rows[0])
+        smooth_rows(act1[:, :, HALF - P :], sm_sb[:, 1, :], 0, rows[1])
 
         pieces = [slice(0, QUARTER), slice(QUARTER, HALF - P), slice(HALF - P, HALF)]
         h8, h4 = h_tiles("10"), h_tiles("11")
@@ -303,9 +313,16 @@ def tile_list_rvq_gelu_mix_gelu_kernel(
         def columns(u, cols):
             return h_second[:, u, cols.start * PACK : cols.stop * PACK]
 
-        for cols in (slice(0, QUARTER), slice(QUARTER, HALF)):
-            smooth_on_vector(columns(0, cols), act0[:, :, cols], 0)
-        quantise_h(h8, pieces[0], columns(0, pieces[0]))
+        first = placed([P, QUARTER * PACK], BF16, "h10_first", ACT0)
+        nc.gpsimd.tensor_tensor(
+            first[:, : P * PACK].rearrange("p (c t) -> p c t", t=PACK),
+            act0[:, :, :P].rearrange("p t c -> p c t"),
+            sm_sb[:, 0, :].unsqueeze(1).to_broadcast([P, P, PACK]),
+            MULT,
+        )
+        smooth_on_vector(columns(0, slice(QUARTER, HALF)), act0[:, :, QUARTER:], 0, sm_psum)
+        smooth_on_vector(first[:, P * PACK :], act0[:, :, P:QUARTER], 0, sm_psum)
+        quantise_h(h8, pieces[0], first[:])
         smooth_on_vector(columns(1, slice(0, P)), act1[:, :, :P], 1)
         interleave(columns(1, slice(P, HALF - P)), rows[0][:])
         quantise_h(later8, slice(QUARTER, HALF), columns(0, slice(QUARTER, HALF)))
@@ -313,6 +330,6 @@ def tile_list_rvq_gelu_mix_gelu_kernel(
         interleave(columns(1, pieces[2]), rows[1][:])
         for cols in pieces[1:]:
             quantise_h(h4, cols, columns(1, cols))
-        second_layer((0, 7), h_first[0], h_first[1], slice(0, HALF), 0, "0")
+        second_layer((5, 6), h_first[0], h_first[1], slice(0, HALF), 0, "0")
         for c, cols in enumerate(pieces):
-            second_layer((1 + 2 * c, 2 + 2 * c), later8 if c else h8, h4, cols, HALF, f"1{c}")
+            second_layer((2 * c, 2 * c + 1), later8 if c else h8, h4, cols, HALF, f"1{c}")

@@ -49,6 +49,7 @@ def tile_list_rvq_gelu_mix_gelu_kernel(
         W0_LOW, ACT0, W0_HIGH = 0, 8 * KB, 15 * KB
         GROUPED, W2S_RAW, ROWS, NO_BIAS = 23 * KB, 27 * KB, 32 * KB, 40 * KB
         SM_WIDE = 44 * KB
+        BESIDE = 48
 
         offsets = keep.tile([P, 3 * J // 16], U16, name="offsets")
         nc.sync.dma_start(offsets[:], offs)
@@ -148,8 +149,6 @@ def tile_list_rvq_gelu_mix_gelu_kernel(
         w0_high = load_w0(1, W0_HIGH)
         wd8_w = kept([P, N], I32, "wd8_w")
         nc.sync.dma_start(wd8_w[:], wd8_words[0].rearrange("p n i -> p (n i)").bitcast(I32))
-        sm_wide = placed([P, PACK], F32, "sm_wide", SM_WIDE)
-        nc.gpsimd.tensor_copy(sm_wide[:], sm_sb[:, 1, :])
         sm_middle = placed([P, PACK], F32, "sm_middle", SM_WIDE + KB)
         nc.gpsimd.tensor_copy(sm_middle[:], sm_sb[:, 1, :])
         wd4_w = kept([P, 2 * N], U8, "wd4_w")
@@ -235,6 +234,14 @@ def tile_list_rvq_gelu_mix_gelu_kernel(
                 MULT,
             )
 
+        def smooth_on_gpsimd(grouped, act, u):
+            nc.gpsimd.tensor_tensor(
+                grouped.rearrange("p (c t) -> p c t", t=PACK),
+                act.rearrange("p t c -> p c t"),
+                sm_sb[:, u, :].unsqueeze(1).to_broadcast([P, act.shape[2], PACK]),
+                MULT,
+            )
+
         def smooth_rows(act, factors, rows_on_gpsimd, rows):
             for t in range(PACK):
                 factor = factors[:, t : t + 1]
@@ -288,10 +295,11 @@ def tile_list_rvq_gelu_mix_gelu_kernel(
         act1 = activate(acc[1], kept([P, PACK, HALF], F32, "act10"))
         rows = [smooth_rows(act0[:], sm_sb[:, 0, :], PACK, placed([P, PACK, HALF], BF16, "smoothed00", W2S_RAW + KB)),
                 smooth_rows(act1[:, :, :QUARTER], sm_middle, 0, placed([P, PACK, QUARTER], BF16, "smoothed10", ROWS))]
-        grouped = [kept([P, HALF * PACK], BF16, "h00"), placed([P, HALF * PACK], BF16, "h01", ACT0)]
+        chained = placed([P, 2 * HALF * PACK], BF16, "chained", ACT0)
+        grouped = [kept([P, HALF * PACK], BF16, "h00"), chained[:, : HALF * PACK]]
         h_first = [(kept([P, HALF], U32, "h_codes00"), placed([P, HALF], U8, "h_scales00", SM_WIDE + KB)), h_tiles("01")]
         interleave(grouped[0][:], rows[0][:])
-        smooth_on_vector(grouped[1][:, QUARTER * PACK :], act1[:, :, QUARTER:], 1)
+        smooth_on_vector(grouped[1][:, QUARTER * PACK :], act1[:, :, QUARTER:], 1, sm_twice)
         interleave(grouped[1][:, : QUARTER * PACK], rows[1][:])
         for u in range(2):
             quantise_h(h_first[u], slice(0, HALF), grouped[u][:])
@@ -300,36 +308,38 @@ def tile_list_rvq_gelu_mix_gelu_kernel(
         first_layer(acc, 1)
         act0 = activate(acc[0], kept([P, PACK, HALF], F32, "act01"))
         last_sum(acc, 1, 1)
-        act1 = activate(acc[1], kept([P, PACK, HALF], F32, "act11"))
-        rows = [kept([P, PACK, QUARTER], BF16, "smoothed_wide"), kept([P, PACK, P], BF16, "smoothed_last")]
-        smooth_rows(act1[:, :, P : HALF - P], sm_wide, 0, rows[0])
-        smooth_rows(act1[:, :, HALF - P :], sm_sb[:, 1, :], 0, rows[1])
-
+        act1 = kept([P, PACK, HALF], F32, "act11")
+        for t in range(PACK - 1):
+            nc.scalar.activation(act1[:, t, :], acc[1][t], GELU)
+        for cols in (slice(0, QUARTER), slice(QUARTER, HALF)):
+            nc.scalar.activation(act1[:, PACK - 1, cols], acc[1][PACK - 1][:, cols], GELU)
         pieces = [slice(0, QUARTER), slice(QUARTER, HALF - P), slice(HALF - P, HALF)]
+        rows = [smooth_rows(act1[:, :, cols], sm_sb[:, 1, :], 0, kept([P, PACK, P], BF16, f"smoothed1{cols.start}"))
+                for cols in pieces[1:]]
+
         h8, h4 = h_tiles("10"), h_tiles("11")
-        later8 = (kept([P, HALF], U32, "h_codes_later"), placed([P, HALF], U8, "h_scales_later", SM_WIDE))
         h_second = placed([P, 2, HALF * PACK], BF16, "h1", ROWS)
 
         def columns(u, cols):
             return h_second[:, u, cols.start * PACK : cols.stop * PACK]
 
-        first = placed([P, QUARTER * PACK], BF16, "h10_first", ACT0)
-        nc.gpsimd.tensor_tensor(
-            first[:, : P * PACK].rearrange("p (c t) -> p c t", t=PACK),
-            act0[:, :, :P].rearrange("p t c -> p c t"),
-            sm_sb[:, 0, :].unsqueeze(1).to_broadcast([P, P, PACK]),
-            MULT,
-        )
+        start = (HALF - P) * PACK
+        first = chained[:, start : start + QUARTER * PACK]
+        smooth_on_gpsimd(first[:, : P * PACK], act0[:, :, :P], 0)
         smooth_on_vector(columns(0, slice(QUARTER, HALF)), act0[:, :, QUARTER:], 0, sm_psum)
         smooth_on_vector(first[:, P * PACK :], act0[:, :, P:QUARTER], 0, sm_psum)
-        quantise_h(h8, pieces[0], first[:])
-        smooth_on_vector(columns(1, slice(0, P)), act1[:, :, :P], 1)
-        interleave(columns(1, slice(P, HALF - P)), rows[0][:])
-        quantise_h(later8, slice(QUARTER, HALF), columns(0, slice(QUARTER, HALF)))
-        quantise_h(h4, pieces[0], columns(1, pieces[0]))
-        interleave(columns(1, pieces[2]), rows[1][:])
-        for cols in pieces[1:]:
-            quantise_h(h4, cols, columns(1, cols))
+        quantise_h(h8, slice(QUARTER, HALF), columns(0, slice(QUARTER, HALF)))
+        quantise_h(h8, pieces[0], first)
+        start += (QUARTER - BESIDE) * PACK
+        upper = chained[:, start : start + QUARTER * PACK]
+        smooth_on_gpsimd(upper[:, : BESIDE * PACK], act1[:, :, :BESIDE], 1)
+        smooth_on_vector(upper[:, BESIDE * PACK :], act1[:, :, BESIDE:QUARTER], 1, sm_psum)
+        waiting = (pieces[0], upper)
+        for cols, smoothed in zip(pieces[1:], rows):
+            interleave(columns(1, cols), smoothed[:])
+            quantise_h(h4, *waiting)
+            waiting = (cols, columns(1, cols))
+        quantise_h(h4, *waiting)
         second_layer((5, 6), h_first[0], h_first[1], slice(0, HALF), 0, "0")
         for c, cols in enumerate(pieces):
-            second_layer((2 * c, 2 * c + 1), later8 if c else h8, h4, cols, HALF, f"1{c}")
+            second_layer((2 * c, 2 * c + 1), h8, h4, cols, HALF, f"1{c}")

@@ -223,7 +223,7 @@ def tile_list_rvq_gelu_mix_gelu_kernel(
                 nc.scalar.activation(act[:, t, :], acc[t], GELU, bias=no_bias[:] if t < with_bias_tile else 0.0)
             return act
 
-        def smooth_on_vector(grouped, act, u, twice=sm_twice):
+        def smooth_on_vector(grouped, act, u, twice):
             width = act.shape[2]
             pairs = twice[:, 2 * u * PACK : 2 * (u + 1) * PACK].rearrange("p (t e) -> p t e", e=2)
             factor = pairs.unsqueeze(1).to_broadcast([P, width // 2, PACK, 2])
@@ -299,7 +299,9 @@ def tile_list_rvq_gelu_mix_gelu_kernel(
         grouped = [kept([P, HALF * PACK], BF16, "h00"), chained[:, : HALF * PACK]]
         h_first = [(kept([P, HALF], U32, "h_codes00"), placed([P, HALF], U8, "h_scales00", SM_WIDE + KB)), h_tiles("01")]
         interleave(grouped[0][:], rows[0][:])
-        smooth_on_vector(grouped[1][:, QUARTER * PACK :], act1[:, :, QUARTER:], 1, sm_twice)
+        split = QUARTER + BESIDE
+        smooth_on_vector(grouped[1][:, split * PACK :], act1[:, :, split:], 1, sm_psum)
+        smooth_on_gpsimd(grouped[1][:, QUARTER * PACK : split * PACK], act1[:, :, QUARTER:split], 1)
         interleave(grouped[1][:, : QUARTER * PACK], rows[1][:])
         for u in range(2):
             quantise_h(h_first[u], slice(0, HALF), grouped[u][:])
@@ -308,13 +310,13 @@ def tile_list_rvq_gelu_mix_gelu_kernel(
         first_layer(acc, 1)
         act0 = activate(acc[0], kept([P, PACK, HALF], F32, "act01"))
         last_sum(acc, 1, 1)
-        act1 = kept([P, PACK, HALF], F32, "act11")
+        act1 = kept([P, 2, PACK, QUARTER], F32, "act11")
         for t in range(PACK - 1):
-            nc.scalar.activation(act1[:, t, :], acc[1][t], GELU)
-        for cols in (slice(0, QUARTER), slice(QUARTER, HALF)):
-            nc.scalar.activation(act1[:, PACK - 1, cols], acc[1][PACK - 1][:, cols], GELU)
+            nc.scalar.activation(act1[:, :, t], acc[1][t].rearrange("p (q c) -> p q c", q=2), GELU)
+        for q in range(2):
+            nc.scalar.activation(act1[:, q, PACK - 1], acc[1][PACK - 1][:, q * QUARTER : (q + 1) * QUARTER], GELU)
         pieces = [slice(0, QUARTER), slice(QUARTER, HALF - P), slice(HALF - P, HALF)]
-        rows = [smooth_rows(act1[:, :, cols], sm_sb[:, 1, :], 0, kept([P, PACK, P], BF16, f"smoothed1{cols.start}"))
+        rows = [smooth_rows(act1[:, 1, :, cols.start - QUARTER : cols.stop - QUARTER], sm_sb[:, 1, :], 0, kept([P, PACK, P], BF16, f"smoothed1{cols.start}"))
                 for cols in pieces[1:]]
 
         h8, h4 = h_tiles("10"), h_tiles("11")
@@ -332,8 +334,8 @@ def tile_list_rvq_gelu_mix_gelu_kernel(
         quantise_h(h8, pieces[0], first)
         start += (QUARTER - BESIDE) * PACK
         upper = chained[:, start : start + QUARTER * PACK]
-        smooth_on_gpsimd(upper[:, : BESIDE * PACK], act1[:, :, :BESIDE], 1)
-        smooth_on_vector(upper[:, BESIDE * PACK :], act1[:, :, BESIDE:QUARTER], 1, sm_psum)
+        smooth_on_gpsimd(upper[:, : BESIDE * PACK], act1[:, 0, :, :BESIDE], 1)
+        smooth_on_vector(upper[:, BESIDE * PACK :], act1[:, 0, :, BESIDE:], 1, sm_psum)
         waiting = (pieces[0], upper)
         for cols, smoothed in zip(pieces[1:], rows):
             interleave(columns(1, cols), smoothed[:])

from contextlib import ExitStack

import concourse.mybir as mybir
from concourse.masks import make_identity

K, R, N, T, J = 512, 1024, 256, 4096, 1024
FLOPS = 2 * (3 * K * R * J + R * N * J)

F32 = mybir.dt.float32
BF16 = mybir.dt.bfloat16
I32 = mybir.dt.int32
U32 = mybir.dt.uint32
U16 = mybir.dt.uint16
U8 = mybir.dt.uint8
FP8X4 = mybir.dt.float8_e4m3fn_x4
FP4X4 = mybir.dt.float4_e2m1fn_x4
GELU = mybir.ActivationFunctionType.Gelu_apprx_tanh
COPY = mybir.ActivationFunctionType.Copy
MULT = mybir.AluOpType.mult
ADD = mybir.AluOpType.add

P = 128
PACK = 4
HALF = 512
QUARTER = 256
KB = 1024


def tile_list_rvq_gelu_mix_gelu_kernel(
    tc, tab_words, tab_scales, w0, w1_words, w1_scales, w2_words, w2_scales, sm,
    wd8_words, wd8_scales, wd4_words, wd4_scales, b, offs, out,
):
    nc = tc.nc
    with ExitStack() as ctx:
        keep = ctx.enter_context(tc.tile_pool(name="keep", bufs=1))
        reused = ctx.enter_context(tc.tile_pool(name="reused", bufs=1))
        psum = ctx.enter_context(tc.psum_pool(name="psum", bufs=1))

        def kept(shape, dtype, name):
            return keep.tile(shape, dtype, name=name, align_bytes=64)

        def placed(shape, dtype, name, offset):
            return reused.tile(shape, dtype, name=name, offset=offset, align_bytes=64)

        def load_scale_rows(scales, plane):
            for r in range(4):
                nc.sync.dma_start(plane[r:P:32, :].bitcast(I32), scales[0, r:16:4, :].bitcast(I32))

        W0_LOW, ACT0, W0_HIGH = 0, 8 * KB, 15 * KB
        GROUPED, W2S_RAW, ROWS, NO_BIAS = 23 * KB, 27 * KB, 32 * KB, 40 * KB
        SM_WIDE = 44 * KB
        BESIDE = 48

        offsets = keep.tile([P, 3 * J // 16], U16, name="offsets")
        nc.sync.dma_start(offsets[:], offs)
        tab_s = kept([P, T], U8, "tab_s")
        nc.vector.memset(tab_s[:].bitcast(I32), 0)
        load_scale_rows(tab_scales, tab_s[:])
        sm_sb = kept([P, 2, PACK], F32, "sm_sb")
        nc.sync.dma_start(sm_sb[:], sm.rearrange("(u p t) -> p u t", u=2, t=PACK))
        w1_raw = kept([P, 2 * R], U8, "w1_raw")
        nc.sync.dma_start(w1_raw[:].bitcast(I32), w1_words[0].bitcast(I32))
        tab_w = kept([P, T], I32, "tab_w")
        nc.sync.dma_start(tab_w[:], tab_words[0].rearrange("p t i -> p (t i)").bitcast(I32))

        w1s_raw = kept([P, R], U8, "w1s_raw")
        nc.vector.memset(w1s_raw[:].bitcast(I32), 0)
        load_scale_rows(w1_scales, w1s_raw[:])
        w2_raw = placed([P, 2 * R], U8, "w2_raw", GROUPED)
        nc.sync.dma_start(w2_raw[:].bitcast(I32), w2_words[0].bitcast(I32))
        w2s_raw = kept([P, R], U8, "w2s_raw")
        nc.vector.memset(w2s_raw[:].bitcast(I32), 0)
        wd_s = kept([P, 2 * N], U8, "wd_s")
        nc.vector.memset(wd_s[:].bitcast(I32), 0)

        sm_twice = kept([P, P], F32, "sm_twice")
        nc.vector.memset(sm_twice[:], 0.0)
        identity = kept([P, P], F32, "identity")
        nc.vector.memset(identity[:], 0.0)
        make_identity(nc, identity[:], nomemset=True)
        nc.gpsimd.tensor_copy(
            sm_twice[:, : 4 * PACK].rearrange("p (c e) -> p c e", e=2),
            sm_sb[:].rearrange("p u t -> p (u t)").unsqueeze(2).to_broadcast([P, 2 * PACK, 2]),
        )
        zero = kept([P, 1], F32, "zero")
        nc.vector.memset(zero[:], 0.0)
        no_bias = placed([P, 1], F32, "no_bias", NO_BIAS)
        nc.scalar.activation(no_bias[:], zero[:], GELU)

        def offsets_of(g, half):
            first = (g * J + half * HALF) // 16
            return offsets[:, first : first + HALF // 16]

        v_s, v_w, w_codes, w_scales = {}, {}, {}, {}

        def gather_scales(g, half, offset=None):
            name = f"picked_s{g}_{half}"
            picked = kept([P, HALF], U8, name) if offset is None else placed([P, HALF], U8, name, offset)
            nc.vector.tensor_copy(picked[:], tab_s[:].indirect(offsets_of(g, half)))
            v_s[g, half] = picked[:]

        def gather_words(g, half, picked):
            nc.vector.tensor_copy(picked, tab_w[:].bitcast(U32).indirect(offsets_of(g, half)))
            v_w[g, half] = picked

        def deal_words(g, u, raw):
            codes = kept([P, 2 * HALF], U8, f"w{g}_codes{u}")
            nc.scalar.copy(
                codes[:].bitcast(U16).rearrange("p (t m) -> p t m", t=PACK),
                raw[:, 2 * u * HALF : 2 * (u + 1) * HALF].bitcast(U16).rearrange("p (m t) -> p t m", t=PACK),
            )
            for t in range(PACK):
                w_codes[g, u, t] = codes[:, 2 * t * P : 2 * (t + 1) * P].bitcast(FP4X4)

        def deal_scales(g, u, raw, plane):
            nc.gpsimd.tensor_copy(
                plane[:].rearrange("p (t m) -> p t m", t=PACK),
                raw[:, u * HALF : (u + 1) * HALF].rearrange("p (m t) -> p t m", t=PACK),
            )
            for t in range(PACK):
                w_scales[g, u, t] = plane[:, t * P : (t + 1) * P]

        w0_rows = w0.rearrange("(p i) r -> p i r", i=PACK)

        def load_w0(u, offset):
            raw = placed([P, 2, PACK, QUARTER], F32, f"w0_raw{u}", offset)
            for c in range(2):
                first = u * HALF + c * QUARTER
                nc.sync.dma_start(raw[:, c], w0_rows[:, :, first : first + QUARTER])
            return raw

        def round_w0(raw, grouped):
            dealt = grouped[:].rearrange("p (a e m i) -> p a m i e", a=2, e=2, i=PACK)
            for c in range(2):
                src = raw[:, c].rearrange("p i (m a e) -> p a m i e", a=2, e=2)
                nc.scalar.copy(dealt[:, :, c * 64 : (c + 1) * 64], src)
            return grouped

        def quantise_w0(u, grouped):
            codes = kept([P, HALF], U32, f"w0_codes{u}")
            plane = kept([P, HALF], U8, f"w0_scales{u}")
            nc.vector.quantize_mx(codes[:].bitcast(FP8X4), plane[:], grouped[:])
            for t in range(PACK):
                w_codes[0, u, t] = codes[:, t * P : (t + 1) * P].bitcast(FP8X4)
                w_scales[0, u, t] = plane[:, t * P : (t + 1) * P]

        w0_low = load_w0(0, W0_LOW)
        load_scale_rows(w2_scales, w2s_raw[:])
        w0_high = load_w0(1, W0_HIGH)
        wd8_w = kept([P, N], I32, "wd8_w")
        nc.sync.dma_start(wd8_w[:], wd8_words[0].rearrange("p n i -> p (n i)").bitcast(I32))
        sm_middle = placed([P, PACK], F32, "sm_middle", SM_WIDE + KB)
        nc.gpsimd.tensor_copy(sm_middle[:], sm_sb[:, 1, :])
        wd4_w = kept([P, 2 * N], U8, "wd4_w")
        nc.sync.dma_start(wd4_w[:].bitcast(I32), wd4_words[0].bitcast(I32))
        wd8_s, wd4_s = wd_s[:, :N], wd_s[:, N:]
        load_scale_rows(wd8_scales, wd8_s)
        load_scale_rows(wd4_scales, wd4_s)
        b_sb = kept([P, 2], F32, "b_sb")
        with nc.allow_non_contiguous_dma(reason="one bias value to a partition"):
            nc.sync.dma_start(b_sb[:], b.rearrange("(n p) -> p n", p=P))

        for g, raw in ((1, w1_raw), (2, w2_raw)):
            for u in range(2):
                deal_words(g, u, raw)
        for g, u, raw in ((1, 0, w1s_raw), (1, 1, w1s_raw), (2, 0, w2s_raw)):
            deal_scales(g, u, raw, kept([P, HALF], U8, f"w{g}_scales{u}"))
        early = kept([P, 3 * HALF], U8, "picked_s_early")
        nc.vector.tensor_copy(early[:], tab_s[:].indirect(offsets[:, J // 16 : (J + 3 * HALF) // 16]))
        for c, place in enumerate(((1, 0), (1, 1), (2, 0))):
            v_s[place] = early[:, c * HALF : (c + 1) * HALF]
        gather_scales(0, 0)
        gather_words(1, 0, kept([P, HALF], U32, "picked_w1_0")[:])
        both = kept([P, J], U32, "picked_w2")
        nc.vector.tensor_copy(both[:], tab_w[:].bitcast(U32).indirect(offsets[:, 2 * J // 16 :]))
        for half in range(2):
            v_w[2, half] = both[:, half * HALF : (half + 1) * HALF]
        gather_words(0, 0, kept([P, HALF], U32, "picked_w0_0")[:])

        def bank(index, width):
            tile = psum.tile([P, HALF], F32, name="bank", tag=f"bank{index}")
            return tile[:, :width]

        turned = bank(6, P)
        nc.tensor.transpose(turned, sm_twice[:], identity[:])
        sm_turned = placed([P, P], F32, "sm_turned", GROUPED + 2 * KB)
        nc.scalar.copy(sm_turned[:], turned)
        sm_psum = bank(7, P)
        nc.tensor.transpose(sm_psum, sm_turned[:], identity[:])

        grouped_low = round_w0(w0_low, placed([P, HALF * PACK], BF16, "w0_grouped0", GROUPED))
        grouped_high = round_w0(w0_high, placed([P, HALF * PACK], BF16, "w0_grouped1", W2S_RAW + KB))
        quantise_w0(0, grouped_low)
        deal_scales(2, 1, w2s_raw, placed([P, HALF], U8, "w2_scales1", GROUPED))
        gather_words(1, 1, placed([P, HALF], U32, "picked_w1_1", W0_LOW)[:])
        quantise_w0(1, grouped_high)
        gather_scales(2, 1, W0_HIGH + KB + HALF)
        gather_scales(0, 1, W0_HIGH + KB)

        def first_layer_pass(acc, g, u, t, half):
            nc.tensor.matmul_mx(
                acc[u][t], lhsT=w_codes[g, u, t], lhsT_scale=w_scales[g, u, t],
                rhs=v_w[g, half].bitcast(FP8X4), rhs_scale=v_s[g, half],
                start=(g == 1), stop=(g == 0),
            )

        def first_layer(acc, half):
            early = half == 0
            for g, u in ((1, 0), (1, 1), (2, 0), (0, 0)) if early else ((1, 0), (2, 0), (0, 0)):
                for t in range(len(acc[u])):
                    first_layer_pass(acc, g, u, t, half)
            for t in range(PACK - 1):
                for g in (2, 0) if early else (1, 2, 0):
                    first_layer_pass(acc, g, 1, t, half)

        def last_sum(acc, half, index):
            acc[1].append(bank(index, HALF))
            for g in (1, 2, 0):
                first_layer_pass(acc, g, 1, PACK - 1, half)

        def activate(acc, act, with_bias_tile=0):
            for t in range(PACK):
                nc.scalar.activation(act[:, t, :], acc[t], GELU, bias=no_bias[:] if t < with_bias_tile else 0.0)
            return act

        def smooth_on_vector(grouped, act, u, twice):
            width = act.shape[2]
            pairs = twice[:, 2 * u * PACK : 2 * (u + 1) * PACK].rearrange("p (t e) -> p t e", e=2)
            factor = pairs.unsqueeze(1).to_broadcast([P, width // 2, PACK, 2])
            nc.vector.tensor_tensor(
                grouped.rearrange("p (c e t) -> p c t e", e=2, t=PACK),
                act.rearrange("p t (c e) -> p c t e", e=2),
                factor,
                MULT,
            )

        def smooth_on_gpsimd(grouped, act, u):
            nc.gpsimd.tensor_tensor(
                grouped.rearrange("p (c t) -> p c t", t=PACK),
                act.rearrange("p t c -> p c t"),
                sm_sb[:, u, :].unsqueeze(1).to_broadcast([P, act.shape[2], PACK]),
                MULT,
            )

        def smooth_rows(act, factors, rows_on_gpsimd, rows):
            for t in range(PACK):
                factor = factors[:, t : t + 1]
                if t < rows_on_gpsimd:
                    nc.gpsimd.tensor_scalar(rows[:, t, :], act[:, t, :], factor, 0.0, MULT, ADD)
                else:
                    nc.scalar.activation(rows[:, t, :], act[:, t, :], COPY, scale=factor)
            return rows

        def interleave(grouped, rows):
            nc.vector.tensor_copy(
                grouped.rearrange("p (c e t) -> p c t e", e=PACK, t=PACK),
                rows.rearrange("p t (c e) -> p c t e", e=PACK),
            )

        def h_tiles(name):
            return kept([P, HALF], U32, f"h_codes{name}"), kept([P, HALF], U8, f"h_scales{name}")

        def quantise_h(h, cols, grouped):
            nc.vector.quantize_mx(h[0][:, cols].bitcast(FP8X4), h[1][:, cols], grouped)

        def second_layer(banks, h8, h4, cols, j_first, name):
            width = cols.stop - cols.start
            step = HALF if width == HALF else P
            sums = [bank(banks[n], width) for n in range(2)]
            for n, y in enumerate(sums):
                nc.tensor.matmul_mx(
                    y, lhsT=wd8_w[:, n * P : (n + 1) * P].bitcast(FP8X4),
                    lhsT_scale=wd8_s[:, n * P : (n + 1) * P],
                    rhs=h8[0][:, cols].bitcast(FP8X4), rhs_scale=h8[1][:, cols],
                    start=True, stop=False,
                )
            for n, y in enumerate(sums):
                for c in range(0, width, step):
                    part = slice(cols.start + c, cols.start + c + step)
                    nc.tensor.matmul_mx(
                        y[:, c : c + step], lhsT=wd4_w[:, 2 * n * P : 2 * (n + 1) * P].bitcast(FP4X4),
                        lhsT_scale=wd4_s[:, n * P : (n + 1) * P],
                        rhs=h4[0][:, part].bitcast(FP8X4), rhs_scale=h4[1][:, part],
                        start=False, stop=(c + step == width),
                    )
                result = kept([P, width], F32, f"result{name}_{n}")
                nc.scalar.activation(result[:], y, GELU, bias=b_sb[:, n : n + 1])
                nc.sync.dma_start(out[n * P : (n + 1) * P, j_first + cols.start : j_first + cols.stop], result[:])

        acc = [[bank(t, HALF) for t in range(PACK)], [bank(PACK + t, HALF) for t in range(PACK - 1)]]
        first_layer(acc, 0)
        act0 = activate(acc[0], placed([P, PACK, HALF], F32, "act00", ACT0), PACK)
        gather_words(0, 1, placed([P, HALF], U32, "picked_late", NO_BIAS)[:])
        last_sum(acc, 0, 0)
        act1 = activate(acc[1], kept([P, PACK, HALF], F32, "act10"))
        rows = [smooth_rows(act0[:], sm_sb[:, 0, :], PACK, placed([P, PACK, HALF], BF16, "smoothed00", W2S_RAW + KB)),
                smooth_rows(act1[:, :, :QUARTER], sm_middle, 0, placed([P, PACK, QUARTER], BF16, "smoothed10", ROWS))]
        chained = placed([P, 2 * HALF * PACK], BF16, "chained", ACT0)
        grouped = [kept([P, HALF * PACK], BF16, "h00"), chained[:, : HALF * PACK]]
        h_first = [(kept([P, HALF], U32, "h_codes00"), placed([P, HALF], U8, "h_scales00", SM_WIDE + KB)), h_tiles("01")]
        interleave(grouped[0][:], rows[0][:])
        split = QUARTER + BESIDE
        smooth_on_vector(grouped[1][:, split * PACK :], act1[:, :, split:], 1, sm_psum)
        smooth_on_gpsimd(grouped[1][:, QUARTER * PACK : split * PACK], act1[:, :, QUARTER:split], 1)
        interleave(grouped[1][:, : QUARTER * PACK], rows[1][:])
        for u in range(2):
            quantise_h(h_first[u], slice(0, HALF), grouped[u][:])

        acc = [[bank(1 + t, HALF) for t in range(PACK)], [bank((5 + t) % 7, HALF) for t in range(PACK - 1)]]
        first_layer(acc, 1)
        act0 = activate(acc[0], kept([P, PACK, HALF], F32, "act01"))
        last_sum(acc, 1, 1)
        act1 = kept([P, 2, PACK, QUARTER], F32, "act11")
        for t in range(PACK - 1):
            nc.scalar.activation(act1[:, :, t], acc[1][t].rearrange("p (q c) -> p q c", q=2), GELU)
        for q in range(2):
            nc.scalar.activation(act1[:, q, PACK - 1], acc[1][PACK - 1][:, q * QUARTER : (q + 1) * QUARTER], GELU)
        pieces = [slice(0, QUARTER), slice(QUARTER, HALF - P), slice(HALF - P, HALF)]
        rows = [smooth_rows(act1[:, 1, :, cols.start - QUARTER : cols.stop - QUARTER], sm_sb[:, 1, :], 0, kept([P, PACK, P], BF16, f"smoothed1{cols.start}"))
                for cols in pieces[1:]]

        h8, h4 = h_tiles("10"), h_tiles("11")
        h_second = placed([P, 2, HALF * PACK], BF16, "h1", ROWS)

        def columns(u, cols):
            return h_second[:, u, cols.start * PACK : cols.stop * PACK]

        start = (HALF - P) * PACK
        first = chained[:, start : start + QUARTER * PACK]
        smooth_on_gpsimd(first[:, : P * PACK], act0[:, :, :P], 0)
        smooth_on_vector(columns(0, slice(QUARTER, HALF)), act0[:, :, QUARTER:], 0, sm_psum)
        smooth_on_vector(first[:, P * PACK :], act0[:, :, P:QUARTER], 0, sm_psum)
        quantise_h(h8, slice(QUARTER, HALF), columns(0, slice(QUARTER, HALF)))
        quantise_h(h8, pieces[0], first)
        start += (QUARTER - BESIDE) * PACK
        upper = chained[:, start : start + QUARTER * PACK]
        smooth_on_gpsimd(upper[:, : BESIDE * PACK], act1[:, 0, :, :BESIDE], 1)
        smooth_on_vector(upper[:, BESIDE * PACK :], act1[:, 0, :, BESIDE:], 1, sm_psum)
        waiting = (pieces[0], upper)
        for cols, smoothed in zip(pieces[1:], rows):
            interleave(columns(1, cols), smoothed[:])
            quantise_h(h4, *waiting)
            waiting = (cols, columns(1, cols))
        quantise_h(h4, *waiting)
        second_layer((5, 6), h_first[0], h_first[1], slice(0, HALF), 0, "0")
        for c, cols in enumerate(pieces):
            second_layer((2 * c, 2 * c + 1), h8, h4, cols, HALF, f"1{c}")
